import numpy as np
import ml_dtypes


def mxq(x, axis, fmt="e4m3"):
    dtype, down = {"e4m3": (ml_dtypes.float8_e4m3fn, 7), "e5m2": (ml_dtypes.float8_e5m2, 14)}[fmt]
    v = np.moveaxis(np.asarray(x, np.float32).astype(ml_dtypes.bfloat16).astype(np.float64), axis, -1)
    blocks = v.reshape(v.shape[:-1] + (-1, 32))
    amax = np.abs(blocks).max(-1, keepdims=True)
    byte = np.maximum(np.where(amax > 0, np.frexp(amax)[1] - 1 + 127, 0) - down, 1)
    scale = np.exp2(byte - 127.0)
    codes = (blocks / scale).astype(np.float32).astype(dtype).astype(np.float64)
    return np.moveaxis((codes * scale).reshape(v.shape), -1, axis)


WIDE = False


def mx_kscale(k):
    if not WIDE:
        return np.ones(k)
    levels = np.array([10, -10, 5, -5, 0])
    if k % 512:
        return np.exp2(np.random.permutation(np.resize(levels, k // 32))).repeat(32)
    a = np.empty((k // 512, 16))
    for p in range(k // 512):
        a[p, :8] = np.random.permutation(np.resize(levels, 8))
        for g in range(8):
            far = levels[np.abs(levels - a[p, g]) >= 10]
            a[p, g + 8] = far[np.random.randint(len(far))]
    return np.exp2(a.ravel()).repeat(32)


def f64(x):
    return np.asarray(x).astype(np.float64)


def striped8(idx):
    return np.asarray(idx).reshape(8, -1, 16).transpose(0, 2, 1).reshape(128, -1).astype(np.uint16)


def unstriped8(offs):
    return offs.reshape(8, 16, -1).transpose(0, 2, 1).reshape(8, -1).astype(np.int64)


def pick8(x, idx, run):
    r = np.arange(len(x))
    return x[r[:, None], idx[r % (8 * run) // run]]


E2M1 = np.array([0.0, 0.5, 1.0, 1.5, 2.0, 3.0, 4.0, 6.0, -0.0, -0.5, -1.0, -1.5, -2.0, -3.0, -4.0, -6.0])


def pack_weight(w, fmt):
    k, n = w.shape
    w = f64(np.asarray(w, np.float32).astype(ml_dtypes.bfloat16)).reshape(k // 32, 32, n)
    amax = np.abs(w).max(1)
    if fmt == "e4m3":
        byte = np.frexp(amax)[1] - 1 + 127 - 7
    else:
        mant, ex = np.frexp(amax / 6.0)
        byte = np.where(mant > 0.5, ex, ex - 1) + 127
    byte = np.clip(np.where(amax > 0, byte, 1), 1, 254)
    scaled = (w * np.exp2(127.0 - byte)[:, None, :]).reshape(k, n).astype(np.float32)
    by_word = np.ascontiguousarray(scaled.reshape(k // 512, 128, 4, n).transpose(0, 1, 3, 2))
    if fmt == "e4m3":
        words = by_word.astype(ml_dtypes.float8_e4m3fn).view(np.uint8)
    else:
        c = by_word.astype(ml_dtypes.float4_e2m1fn).view(np.uint8) & 0xF
        words = (c[..., 0::2] | (c[..., 1::2] << 4)).reshape(k // 512, 128, 2 * n)
    return np.ascontiguousarray(words), np.ascontiguousarray(byte.astype(np.uint8).reshape(k // 512, 16, n))


def unpack_weight(words, scales, fmt):
    g, _, n = scales.shape
    words = np.ascontiguousarray(words).reshape(g, 128, n, -1)
    if fmt == "e4m3":
        vals = words.view(ml_dtypes.float8_e4m3fn).astype(np.float64)
    else:
        nib = np.empty((g, 128, n, 4), np.uint8)
        nib[..., 0::2] = words & 0xF
        nib[..., 1::2] = words >> 4
        vals = E2M1[nib]
    vals = vals * np.repeat(np.exp2(scales.astype(np.float64) - 127.0), 8, axis=1)[..., None]
    return vals.transpose(0, 1, 3, 2).reshape(g * 512, n)


D, T, Q, I, E = 512, 1024, 128, 512, 512


def setup_inputs():
    n = np.random.standard_normal
    idx = np.stack([np.random.permutation(T)[:I] for _ in range(8)])
    fd = mx_kscale(D)
    ft = mx_kscale(T)
    keysp = pack_weight(n((D, T)) / fd[:, None], "e4m3")
    return {
        "query": (n((D, Q)) * 0.2 / np.sqrt(D) * fd[:, None]).astype(np.float32),
        "keys_words": keysp[0],
        "keys_scales": keysp[1],
        "fac": (np.random.uniform(4.0, 16.0, (1, T)) * ft).astype(np.float32),
        "vals": (n((T, E)) / ft[:, None]).astype(np.float32),
        "offs": striped8(idx),
    }


def reference(query, keys_words, keys_scales, fac, vals, offs):
    idx = unstriped8(offs)
    keysu = unpack_weight(keys_words, keys_scales, "e4m3")
    queryq = mxq(f64(query), 0, "e4m3")
    a = queryq.T @ keysu
    b = pick8(a, idx, 16)
    p = np.exp(b - np.max(b, axis=1, keepdims=True))
    w = p / np.sum(p, axis=1, keepdims=True)
    wf = np.zeros((Q, T))
    wf[np.arange(Q)[:, None], idx[np.arange(Q) % 128 // 16]] = w
    wg = wf * f64(fac)
    wt = wg.T
    wtq = mxq(wt, 0, "e4m3")
    valsq = mxq(f64(vals), 0, "e4m3")
    o = wtq.T @ valsq
    return o

@@ -1,0 +1,189 @@
+from contextlib import ExitStack
+
+import concourse.mybir as mybir
+from concourse.masks import make_identity
+
+D, T, Q, SLOTS, E = 512, 1024, 128, 512, 512
+FLOPS = 2 * Q * D * T + 2 * Q * T * E
+
+F32 = mybir.dt.float32
+BF16 = mybir.dt.bfloat16
+I32 = mybir.dt.int32
+U32 = mybir.dt.uint32
+U16 = mybir.dt.uint16
+U8 = mybir.dt.uint8
+FP8X4 = mybir.dt.float8_e4m3fn_x4
+ALU = mybir.AluOpType
+ACT = mybir.ActivationFunctionType
+AXIS_X = mybir.AxisListType.X
+
+P = 128
+PACK = 4
+K_PASS = P * PACK
+PASSES = T // K_PASS
+QUARTER = T // 4
+HALF_E = E // 2
+FIRST = 128
+
+
+def tile_attend_mqa_ownlists_kernel(tc, query, keys_words, keys_scales, fac, vals, offs, out):
+    nc = tc.nc
+    with ExitStack() as ctx:
+        sb = ctx.enter_context(tc.tile_pool(name="sb", bufs=1))
+        ps = ctx.enter_context(tc.psum_pool(name="ps", bufs=1))
+
+        offsets = sb.tile([P, SLOTS // 16], U16, name="offsets")
+        q_raw = sb.tile([P, PACK, Q], F32, name="q_raw")
+        k_words = [sb.tile([P, T // 2], U32, name="k_words%d" % h, align_bytes=64) for h in range(2)]
+        k_scales = sb.tile([P, QUARTER], U8, name="k_scales", align_bytes=64)
+        fac_cols = sb.tile([P, PASSES, PACK], F32, name="fac_cols")
+        placed = sb.tile([P, T], F32, name="placed")
+        ident = sb.tile([P, P], F32, name="ident")
+
+        nc.vector.memset(k_scales[:].bitcast(I32), 0)
+        nc.sync.dma_start(out=q_raw[:], in_=query.rearrange("(p j) q -> p j q", j=PACK))
+        key_ints = keys_words[0].rearrange("p n t -> p (n t)").bitcast(I32)
+        nc.sync.dma_start(out=k_words[0][:].bitcast(I32), in_=key_ints[:, : T // 2])
+        nc.sync.dma_start(offsets[:], offs)
+        scale_words = keys_scales[0].bitcast(I32)
+        for quad in range(4):
+            nc.sync.dma_start(
+                out=k_scales[32 * quad : 32 * quad + 16, :].bitcast(I32),
+                in_=scale_words[4 * quad : 4 * quad + 4, :].rearrange("r (h c) -> h r c", h=4),
+            )
+        nc.sync.dma_start(out=k_words[1][:].bitcast(I32), in_=key_ints[:, T // 2 :])
+        v_raw = {}
+        for g in range(PASSES):
+            for h in range(2):
+                v_raw[g, h] = sb.tile([P, PACK, HALF_E], F32, name="v_raw%d%d" % (g, h))
+                rows = vals[g * K_PASS : (g + 1) * K_PASS, h * HALF_E : (h + 1) * HALF_E]
+                nc.sync.dma_start(out=v_raw[g, h][:], in_=rows.rearrange("(p j) e -> p j e", j=PACK))
+        nc.gpsimd.dma_start(out=fac_cols[:], in_=fac[0].rearrange("(g p j) -> p g j", g=PASSES, j=PACK))
+        make_identity(nc, ident[:])
+        nc.vector.memset(placed[:], 0.0)
+
+        q_bf = sb.tile([P, Q, PACK], BF16, name="q_bf", align_bytes=64)
+        q_codes = sb.tile([P, Q], U32, name="q_codes", align_bytes=64)
+        q_scales = sb.tile([P, Q], U8, name="q_scales", align_bytes=64)
+        nc.vector.tensor_copy(
+            out=q_bf[:].rearrange("p (c i) j -> p c j i", i=4),
+            in_=q_raw[:].rearrange("p j (c i) -> p c j i", i=4),
+        )
+        nc.vector.quantize_mx(
+            out=q_codes[:].bitcast(FP8X4), scales=q_scales[:], in_=q_bf[:].rearrange("p q j -> p (q j)")
+        )
+
+        scores = sb.tile([P, T], F32, name="scores")
+        for n in range(4):
+            cols = slice(n * QUARTER, (n + 1) * QUARTER)
+            bank = ps.tile([P, QUARTER], F32, name="score_bank%d" % n, tag="bank%d" % n)
+            nc.tensor.matmul_mx(
+                out=bank[:],
+                lhsT=q_codes[:].bitcast(FP8X4),
+                lhsT_scale=q_scales[:],
+                rhs=k_words[n // 2][:, (n % 2) * QUARTER : (n % 2 + 1) * QUARTER].bitcast(FP8X4),
+                rhs_scale=k_scales[4 * n : P, :],
+                start=True,
+                stop=True,
+            )
+            if n % 2 == 0:
+                nc.scalar.copy(out=scores[:, cols], in_=bank[:])
+            else:
+                nc.vector.tensor_copy(out=scores[:, cols], in_=bank[:])
+
+        picked = sb.tile([P, SLOTS], F32, name="picked")
+        nc.vector.tensor_copy(picked[:], scores[:].indirect(offsets[:]))
+        neg_max = sb.tile([P, 1], F32, name="neg_max")
+        nc.vector.tensor_reduce(out=neg_max[:], in_=picked[:], axis=AXIS_X, op=ALU.max, negate=True)
+
+        p_first = sb.tile([P, FIRST], F32, name="p_first")
+        p_rest = sb.tile([P, SLOTS - FIRST], F32, name="p_rest")
+        sum_first = sb.tile([P, 1], F32, name="sum_first")
+        sum_rest = sb.tile([P, 1], F32, name="sum_rest")
+        total = sb.tile([P, 1], F32, name="total")
+        inv_total = sb.tile([P, 1], F32, name="inv_total")
+        nc.scalar.activation(
+            out=p_first[:], in_=picked[:, :FIRST], func=ACT.Exp, bias=neg_max[:], accum_out=sum_first[:]
+        )
+        nc.scalar.activation(
+            out=p_rest[:], in_=picked[:, FIRST:], func=ACT.Exp, bias=neg_max[:], accum_out=sum_rest[:]
+        )
+        nc.scalar.activation(out=total[:], in_=sum_first[:], func=ACT.Identity, bias=sum_rest[:])
+
+        nc.vector.tensor_copy(placed[:].indirect(offsets[:, 0:8]), p_first[:])
+        nc.vector.tensor_copy(placed[:].indirect(offsets[:, 8:24]), p_rest[:, 0:256])
+        nc.vector.reciprocal(out=inv_total[:], in_=total[:])
+        nc.vector.tensor_copy(placed[:].indirect(offsets[:, 24:32]), p_rest[:, 256:384])
+
+        fac_rows = []
+        for g in range(PASSES):
+            rows_g = ps.tile([P, PACK, P], F32, name="fac_rows%d" % g, tag="bank%d" % g)
+            for j in range(PACK):
+                nc.tensor.transpose(rows_g[:, j, :], fac_cols[:, g, j : j + 1].to_broadcast([P, P]), ident[:])
+            fac_rows.append(rows_g)
+
+        w_codes = []
+        w_scales = []
+        placed_v = placed[:].rearrange("q (g p u e) -> q g u p e", g=PASSES, u=2, e=2)
+        for g in range(PASSES):
+            turned = ps.tile([P, 2, Q], F32, name="turned%d" % g, tag="bank%d" % (2 + g))
+            fac_v = fac_rows[g][:].rearrange("q (u e) p -> q u p e", e=2)
+            for u in range(2):
+                w_pairs = sb.tile([P, P, 2], BF16, name="w_pairs%d%d" % (g, u))
+                nc.vector.scalar_tensor_tensor(
+                    out=w_pairs[:],
+                    in0=placed_v[:, g, u],
+                    scalar=inv_total[:],
+                    in1=fac_v[:, u],
+                    op0=ALU.mult,
+                    op1=ALU.mult,
+                )
+                nc.tensor.transpose(
+                    turned[:, u, :], w_pairs[:].rearrange("q p e -> q (p e)").bitcast(F32), ident[:]
+                )
+            w_bf = sb.tile([P, Q * PACK], BF16, name="w_bf%d" % g, align_bytes=64)
+            nc.scalar.copy(
+                out=w_bf[:].bitcast(F32).rearrange("p (q u) -> p q u", u=2),
+                in_=turned[:].rearrange("p u q -> p q u"),
+            )
+            codes_g = sb.tile([P, Q], U32, name="w_codes%d" % g, align_bytes=64)
+            scales_g = sb.tile([P, Q], U8, name="w_scales%d" % g, align_bytes=64)
+            nc.vector.quantize_mx(out=codes_g[:].bitcast(FP8X4), scales=scales_g[:], in_=w_bf[:])
+            w_codes.append(codes_g)
+            w_scales.append(scales_g)
+
+        v_codes = {}
+        v_scales = {}
+        for g in range(PASSES):
+            for h in range(2):
+                v_bf = sb.tile([P, HALF_E, PACK], BF16, name="v_bf%d%d" % (g, h), align_bytes=64)
+                nc.scalar.copy(
+                    out=v_bf[:].rearrange("p (c i) j -> p c j i", i=4),
+                    in_=v_raw[g, h][:].rearrange("p j (c i) -> p c j i", i=4),
+                )
+                v_codes[g, h] = sb.tile([P, HALF_E], U32, name="v_codes%d%d" % (g, h), align_bytes=64)
+                v_scales[g, h] = sb.tile([P, HALF_E], U8, name="v_scales%d%d" % (g, h), align_bytes=64)
+                nc.vector.quantize_mx(
+                    out=v_codes[g, h][:].bitcast(FP8X4),
+                    scales=v_scales[g, h][:],
+                    in_=v_bf[:].rearrange("p e j -> p (e j)"),
+                )
+
+        acc = [ps.tile([P, HALF_E], F32, name="acc%d" % h) for h in range(2)]
+        for g in range(PASSES):
+            for h in range(2):
+                nc.tensor.matmul_mx(
+                    out=acc[h][:],
+                    lhsT=w_codes[g][:].bitcast(FP8X4),
+                    lhsT_scale=w_scales[g][:],
+                    rhs=v_codes[g, h][:].bitcast(FP8X4),
+                    rhs_scale=v_scales[g, h][:],
+                    start=(g == 0),
+                    stop=(g == PASSES - 1),
+                )
+        result0 = sb.tile([P, HALF_E], F32, name="result0")
+        result1 = sb.tile([P, HALF_E], F32, name="result1")
+        nc.scalar.copy(out=result0[:], in_=acc[0][:])
+        nc.vector.tensor_copy(out=result1[:], in_=acc[1][:])
+        nc.sync.dma_start(out=out[:, :HALF_E], in_=result0[:])
+        nc.scalar.dma_start(out=out[:, HALF_E:], in_=result1[:])

@@ -24,6 +24,10 @@ PASSES = T // K_PASS
 QUARTER = T // 4
 HALF_E = E // 2
 FIRST = 128
+Q_VECTOR = 88
+SCORE_WIDTHS = (256, 256, 128, 128, 128, 128)
+OUT_WIDTH = 128
+EARLY_UNITS = 2
 
 
 def tile_attend_mqa_ownlists_kernel(tc, query, keys_words, keys_scales, fac, vals, offs, out):
@@ -33,11 +37,10 @@ def tile_attend_mqa_ownlists_kernel(tc, query, keys_words, keys_scales, fac, val
         ps = ctx.enter_context(tc.psum_pool(name="ps", bufs=1))
 
         offsets = sb.tile([P, SLOTS // 16], U16, name="offsets")
-        q_raw = sb.tile([P, PACK, Q], F32, name="q_raw")
+        q_raw = sb.tile([P, PACK, Q], F32, name="q_raw", tag="q_raw")
         k_words = [sb.tile([P, T // 2], U32, name="k_words%d" % h, align_bytes=64) for h in range(2)]
         k_scales = sb.tile([P, QUARTER], U8, name="k_scales", align_bytes=64)
         fac_cols = sb.tile([P, PASSES, PACK], F32, name="fac_cols")
-        placed = sb.tile([P, T], F32, name="placed")
         ident = sb.tile([P, P], F32, name="ident")
 
         nc.vector.memset(k_scales[:].bitcast(I32), 0)
@@ -55,34 +58,43 @@ def tile_attend_mqa_ownlists_kernel(tc, query, keys_words, keys_scales, fac, val
         v_raw = {}
         for g in range(PASSES):
             for h in range(2):
-                v_raw[g, h] = sb.tile([P, PACK, HALF_E], F32, name="v_raw%d%d" % (g, h))
+                v_raw[g, h] = sb.tile([P, PACK, HALF_E], F32, name="v_raw%d%d" % (g, h), tag="v_raw%d%d" % (g, h), align_bytes=64)
                 rows = vals[g * K_PASS : (g + 1) * K_PASS, h * HALF_E : (h + 1) * HALF_E]
                 nc.sync.dma_start(out=v_raw[g, h][:], in_=rows.rearrange("(p j) e -> p j e", j=PACK))
         nc.gpsimd.dma_start(out=fac_cols[:], in_=fac[0].rearrange("(g p j) -> p g j", g=PASSES, j=PACK))
         make_identity(nc, ident[:])
-        nc.vector.memset(placed[:], 0.0)
 
         q_bf = sb.tile([P, Q, PACK], BF16, name="q_bf", align_bytes=64)
         q_codes = sb.tile([P, Q], U32, name="q_codes", align_bytes=64)
         q_scales = sb.tile([P, Q], U8, name="q_scales", align_bytes=64)
         nc.vector.tensor_copy(
-            out=q_bf[:].rearrange("p (c i) j -> p c j i", i=4),
-            in_=q_raw[:].rearrange("p j (c i) -> p c j i", i=4),
+            out=q_bf[:, :Q_VECTOR, :].rearrange("p (c i) j -> p c j i", i=4),
+            in_=q_raw[:, :, :Q_VECTOR].rearrange("p j (c i) -> p c j i", i=4),
+        )
+        nc.scalar.copy(
+            out=q_bf[:, Q_VECTOR:, :].rearrange("p (c i) j -> p c j i", i=4),
+            in_=q_raw[:, :, Q_VECTOR:].rearrange("p j (c i) -> p c j i", i=4),
         )
         nc.vector.quantize_mx(
             out=q_codes[:].bitcast(FP8X4), scales=q_scales[:], in_=q_bf[:].rearrange("p q j -> p (q j)")
         )
 
+        placed = sb.tile([P, T], F32, name="placed", tag="q_raw")
+        nc.vector.memset(placed[:], 0.0)
+
         scores = sb.tile([P, T], F32, name="scores")
-        for n in range(4):
-            cols = slice(n * QUARTER, (n + 1) * QUARTER)
-            bank = ps.tile([P, QUARTER], F32, name="score_bank%d" % n, tag="bank%d" % n)
+        start = 0
+        for n, width in enumerate(SCORE_WIDTHS):
+            cols = slice(start, start + width)
+            quarter, in_quarter = divmod(start, QUARTER)
+            half, in_half = divmod(start, T // 2)
+            bank = ps.tile([P, width], F32, name="score_bank%d" % n, tag="bank%d" % n)
             nc.tensor.matmul_mx(
                 out=bank[:],
                 lhsT=q_codes[:].bitcast(FP8X4),
                 lhsT_scale=q_scales[:],
-                rhs=k_words[n // 2][:, (n % 2) * QUARTER : (n % 2 + 1) * QUARTER].bitcast(FP8X4),
-                rhs_scale=k_scales[4 * n : P, :],
+                rhs=k_words[half][:, in_half : in_half + width].bitcast(FP8X4),
+                rhs_scale=k_scales[4 * quarter : P, in_quarter : in_quarter + width],
                 start=True,
                 stop=True,
             )
@@ -90,8 +102,9 @@ def tile_attend_mqa_ownlists_kernel(tc, query, keys_words, keys_scales, fac, val
                 nc.scalar.copy(out=scores[:, cols], in_=bank[:])
             else:
                 nc.vector.tensor_copy(out=scores[:, cols], in_=bank[:])
+            start = start + width
 
-        picked = sb.tile([P, SLOTS], F32, name="picked")
+        picked = sb.tile([P, SLOTS], F32, name="picked", tag="picked", align_bytes=64)
         nc.vector.tensor_copy(picked[:], scores[:].indirect(offsets[:]))
         neg_max = sb.tile([P, 1], F32, name="neg_max")
         nc.vector.tensor_reduce(out=neg_max[:], in_=picked[:], axis=AXIS_X, op=ALU.max, negate=True)
@@ -101,7 +114,7 @@ def tile_attend_mqa_ownlists_kernel(tc, query, keys_words, keys_scales, fac, val
         sum_first = sb.tile([P, 1], F32, name="sum_first")
         sum_rest = sb.tile([P, 1], F32, name="sum_rest")
         total = sb.tile([P, 1], F32, name="total")
-        inv_total = sb.tile([P, 1], F32, name="inv_total")
+        inv_total = sb.tile([P, 1], F32, name="inv_total", tag="inv_total", align_bytes=64)
         nc.scalar.activation(
             out=p_first[:], in_=picked[:, :FIRST], func=ACT.Exp, bias=neg_max[:], accum_out=sum_first[:]
         )
@@ -111,9 +124,8 @@ def tile_attend_mqa_ownlists_kernel(tc, query, keys_words, keys_scales, fac, val
         nc.scalar.activation(out=total[:], in_=sum_first[:], func=ACT.Identity, bias=sum_rest[:])
 
         nc.vector.tensor_copy(placed[:].indirect(offsets[:, 0:8]), p_first[:])
-        nc.vector.tensor_copy(placed[:].indirect(offsets[:, 8:24]), p_rest[:, 0:256])
+        nc.vector.tensor_copy(placed[:].indirect(offsets[:, 8:32]), p_rest[:])
         nc.vector.reciprocal(out=inv_total[:], in_=total[:])
-        nc.vector.tensor_copy(placed[:].indirect(offsets[:, 24:32]), p_rest[:, 256:384])
 
         fac_rows = []
         for g in range(PASSES):
@@ -122,11 +134,10 @@ def tile_attend_mqa_ownlists_kernel(tc, query, keys_words, keys_scales, fac, val
                 nc.tensor.transpose(rows_g[:, j, :], fac_cols[:, g, j : j + 1].to_broadcast([P, P]), ident[:])
             fac_rows.append(rows_g)
 
-        w_codes = []
-        w_scales = []
         placed_v = placed[:].rearrange("q (g p u e) -> q g u p e", g=PASSES, u=2, e=2)
+        turned = []
         for g in range(PASSES):
-            turned = ps.tile([P, 2, Q], F32, name="turned%d" % g, tag="bank%d" % (2 + g))
+            turned_g = ps.tile([P, 2, Q], F32, name="turned%d" % g, tag="bank%d" % (2 + g))
             fac_v = fac_rows[g][:].rearrange("q (u e) p -> q u p e", e=2)
             for u in range(2):
                 w_pairs = sb.tile([P, P, 2], BF16, name="w_pairs%d%d" % (g, u))
@@ -139,51 +150,69 @@ def tile_attend_mqa_ownlists_kernel(tc, query, keys_words, keys_scales, fac, val
                     op1=ALU.mult,
                 )
                 nc.tensor.transpose(
-                    turned[:, u, :], w_pairs[:].rearrange("q p e -> q (p e)").bitcast(F32), ident[:]
+                    turned_g[:, u, :], w_pairs[:].rearrange("q p e -> q (p e)").bitcast(F32), ident[:]
                 )
-            w_bf = sb.tile([P, Q * PACK], BF16, name="w_bf%d" % g, align_bytes=64)
+            turned.append(turned_g)
+
+        units = [(g, n) for g in range(PASSES) for n in range(4)]
+        v_codes = sb.tile([P, len(units) * OUT_WIDTH], U32, name="v_codes", align_bytes=64)
+        early_scales = sb.tile([P, EARLY_UNITS * OUT_WIDTH], U8, name="early_scales", align_bytes=64)
+        late_scales = sb.tile(
+            [P, (len(units) - EARLY_UNITS) * OUT_WIDTH], U8, name="late_scales", tag="inv_total", align_bytes=64
+        )
+        unit_codes = {}
+        unit_scales = {}
+        for i, (g, n) in enumerate(units):
+            h, in_half = divmod(n * OUT_WIDTH, HALF_E)
+            if i % 2 == 0:
+                bf_tag = "picked" if i == EARLY_UNITS else "v_bf%d" % i
+                v_pair = sb.tile([P, 2, OUT_WIDTH, PACK], BF16, name="v_bf%d" % i, tag=bf_tag, align_bytes=64)
+            v_bf = v_pair[:, i % 2]
+            nc.scalar.copy(
+                out=v_bf.rearrange("p (c i) j -> p c j i", i=4),
+                in_=v_raw[g, h][:, :, in_half : in_half + OUT_WIDTH].rearrange("p j (c i) -> p c j i", i=4),
+            )
+            unit_codes[g, n] = v_codes[:, i * OUT_WIDTH : (i + 1) * OUT_WIDTH]
+            if i < EARLY_UNITS:
+                unit_scales[g, n] = early_scales[:, i * OUT_WIDTH : (i + 1) * OUT_WIDTH]
+            else:
+                late = i - EARLY_UNITS
+                unit_scales[g, n] = late_scales[:, late * OUT_WIDTH : (late + 1) * OUT_WIDTH]
+            nc.vector.quantize_mx(
+                out=unit_codes[g, n].bitcast(FP8X4),
+                scales=unit_scales[g, n],
+                in_=v_bf.rearrange("p e j -> p (e j)"),
+            )
+
+        w_codes = []
+        w_scales = []
+        for g in range(PASSES):
+            bf_tag = "v_raw11" if g == 0 else "w_bf1"
+            w_bf = sb.tile([P, Q * PACK], BF16, name="w_bf%d" % g, tag=bf_tag, align_bytes=64)
             nc.scalar.copy(
                 out=w_bf[:].bitcast(F32).rearrange("p (q u) -> p q u", u=2),
-                in_=turned[:].rearrange("p u q -> p q u"),
+                in_=turned[g][:].rearrange("p u q -> p q u"),
             )
-            codes_g = sb.tile([P, Q], U32, name="w_codes%d" % g, align_bytes=64)
+            codes_g = sb.tile([P, Q], U32, name="w_codes%d" % g, tag="v_bf6" if g == 0 else "w_codes1", align_bytes=64)
             scales_g = sb.tile([P, Q], U8, name="w_scales%d" % g, align_bytes=64)
             nc.vector.quantize_mx(out=codes_g[:].bitcast(FP8X4), scales=scales_g[:], in_=w_bf[:])
             w_codes.append(codes_g)
             w_scales.append(scales_g)
 
-        v_codes = {}
-        v_scales = {}
+        acc = [ps.tile([P, OUT_WIDTH], F32, name="acc%d" % n, tag="bank%d" % (4 + n)) for n in range(4)]
         for g in range(PASSES):
-            for h in range(2):
-                v_bf = sb.tile([P, HALF_E, PACK], BF16, name="v_bf%d%d" % (g, h), align_bytes=64)
-                nc.scalar.copy(
-                    out=v_bf[:].rearrange("p (c i) j -> p c j i", i=4),
-                    in_=v_raw[g, h][:].rearrange("p j (c i) -> p c j i", i=4),
-                )
-                v_codes[g, h] = sb.tile([P, HALF_E], U32, name="v_codes%d%d" % (g, h), align_bytes=64)
-                v_scales[g, h] = sb.tile([P, HALF_E], U8, name="v_scales%d%d" % (g, h), align_bytes=64)
-                nc.vector.quantize_mx(
-                    out=v_codes[g, h][:].bitcast(FP8X4),
-                    scales=v_scales[g, h][:],
-                    in_=v_bf[:].rearrange("p e j -> p (e j)"),
-                )
-
-        acc = [ps.tile([P, HALF_E], F32, name="acc%d" % h) for h in range(2)]
-        for g in range(PASSES):
-            for h in range(2):
+            for n in range(4):
                 nc.tensor.matmul_mx(
-                    out=acc[h][:],
+                    out=acc[n][:],
                     lhsT=w_codes[g][:].bitcast(FP8X4),
                     lhsT_scale=w_scales[g][:],
-                    rhs=v_codes[g, h][:].bitcast(FP8X4),
-                    rhs_scale=v_scales[g, h][:],
+                    rhs=unit_codes[g, n].bitcast(FP8X4),
+                    rhs_scale=unit_scales[g, n],
                     start=(g == 0),
                     stop=(g == PASSES - 1),
                 )
-        result0 = sb.tile([P, HALF_E], F32, name="result0")
-        result1 = sb.tile([P, HALF_E], F32, name="result1")
-        nc.scalar.copy(out=result0[:], in_=acc[0][:])
-        nc.vector.tensor_copy(out=result1[:], in_=acc[1][:])
-        nc.sync.dma_start(out=out[:, :HALF_E], in_=result0[:])
-        nc.scalar.dma_start(out=out[:, HALF_E:], in_=result1[:])
+        for h in range(2):
+            result = sb.tile([P, HALF_E], F32, name="result%d" % h)
+            nc.scalar.copy(out=result[:, :OUT_WIDTH], in_=acc[2 * h][:])
+            nc.vector.tensor_copy(out=result[:, OUT_WIDTH:], in_=acc[2 * h + 1][:])
+            nc.sync.dma_start(out=out[:, h * HALF_E : (h + 1) * HALF_E], in_=result[:])

@@ -47,7 +47,6 @@ def tile_attend_mqa_ownlists_kernel(tc, query, keys_words, keys_scales, fac, val
         nc.sync.dma_start(out=q_raw[:], in_=query.rearrange("(p j) q -> p j q", j=PACK))
         key_ints = keys_words[0].rearrange("p n t -> p (n t)").bitcast(I32)
         nc.sync.dma_start(out=k_words[0][:].bitcast(I32), in_=key_ints[:, : T // 2])
-        nc.sync.dma_start(offsets[:], offs)
         scale_words = keys_scales[0].bitcast(I32)
         for quad in range(4):
             nc.sync.dma_start(
@@ -55,13 +54,14 @@ def tile_attend_mqa_ownlists_kernel(tc, query, keys_words, keys_scales, fac, val
                 in_=scale_words[4 * quad : 4 * quad + 4, :].rearrange("r (h c) -> h r c", h=4),
             )
         nc.sync.dma_start(out=k_words[1][:].bitcast(I32), in_=key_ints[:, T // 2 :])
+        nc.sync.dma_start(offsets[:], offs)
         v_raw = {}
         for g in range(PASSES):
             for h in range(2):
                 v_raw[g, h] = sb.tile([P, PACK, HALF_E], F32, name="v_raw%d%d" % (g, h), tag="v_raw%d%d" % (g, h), align_bytes=64)
                 rows = vals[g * K_PASS : (g + 1) * K_PASS, h * HALF_E : (h + 1) * HALF_E]
                 nc.sync.dma_start(out=v_raw[g, h][:], in_=rows.rearrange("(p j) e -> p j e", j=PACK))
-        nc.gpsimd.dma_start(out=fac_cols[:], in_=fac[0].rearrange("(g p j) -> p g j", g=PASSES, j=PACK))
+        nc.sync.dma_start(out=fac_cols[:], in_=fac[0].rearrange("(g p j) -> p g j", g=PASSES, j=PACK))
         make_identity(nc, ident[:])
 
         q_bf = sb.tile([P, Q, PACK], BF16, name="q_bf", align_bytes=64)

@@ -26,22 +26,34 @@ HALF_E = E // 2
 FIRST = 128
 Q_VECTOR = 88
 SCORE_WIDTHS = (256, 256, 128, 128, 128, 128)
+SCALAR_BANKS = (0, 2)
 OUT_WIDTH = 128
-EARLY_UNITS = 2
+UNITS = PASSES * E // OUT_WIDTH
+EARLY_UNITS = 3
 
 
 def tile_attend_mqa_ownlists_kernel(tc, query, keys_words, keys_scales, fac, vals, offs, out):
     nc = tc.nc
     with ExitStack() as ctx:
         sb = ctx.enter_context(tc.tile_pool(name="sb", bufs=1))
+        tail = ctx.enter_context(tc.tile_pool(name="tail", bufs=1))
         ps = ctx.enter_context(tc.psum_pool(name="ps", bufs=1))
 
         offsets = sb.tile([P, SLOTS // 16], U16, name="offsets")
-        q_raw = sb.tile([P, PACK, Q], F32, name="q_raw", tag="q_raw")
+        q_raw = sb.tile([P, PACK, Q], F32, name="q_raw")
         k_words = [sb.tile([P, T // 2], U32, name="k_words%d" % h, align_bytes=64) for h in range(2)]
         k_scales = sb.tile([P, QUARTER], U8, name="k_scales", align_bytes=64)
         fac_cols = sb.tile([P, PASSES, PACK], F32, name="fac_cols")
         ident = sb.tile([P, P], F32, name="ident")
+        minus_one = sb.tile([P, 1], F32, name="minus_one")
+        placed = sb.tile([P, T], F32, name="placed")
+        v_raw = [sb.tile([P, PACK, HALF_E], F32, name="v_raw%d" % n) for n in range(3)]
+        v_raw.append(tail.tile([P, PACK, HALF_E], F32, name="v_raw3", offset=0, align_bytes=64))
+
+        def load_values(n):
+            g, h = divmod(n, 2)
+            rows = vals[g * K_PASS : (g + 1) * K_PASS, h * HALF_E : (h + 1) * HALF_E]
+            nc.sync.dma_start(out=v_raw[n][:], in_=rows.rearrange("(p j) e -> p j e", j=PACK))
 
         nc.vector.memset(k_scales[:].bitcast(I32), 0)
         nc.sync.dma_start(out=q_raw[:], in_=query.rearrange("(p j) q -> p j q", j=PACK))
@@ -54,15 +66,15 @@ def tile_attend_mqa_ownlists_kernel(tc, query, keys_words, keys_scales, fac, val
                 in_=scale_words[4 * quad : 4 * quad + 4, :].rearrange("r (h c) -> h r c", h=4),
             )
         nc.sync.dma_start(out=k_words[1][:].bitcast(I32), in_=key_ints[:, T // 2 :])
+        load_values(0)
         nc.sync.dma_start(offsets[:], offs)
-        v_raw = {}
-        for g in range(PASSES):
-            for h in range(2):
-                v_raw[g, h] = sb.tile([P, PACK, HALF_E], F32, name="v_raw%d%d" % (g, h), tag="v_raw%d%d" % (g, h), align_bytes=64)
-                rows = vals[g * K_PASS : (g + 1) * K_PASS, h * HALF_E : (h + 1) * HALF_E]
-                nc.sync.dma_start(out=v_raw[g, h][:], in_=rows.rearrange("(p j) e -> p j e", j=PACK))
+        load_values(1)
         nc.sync.dma_start(out=fac_cols[:], in_=fac[0].rearrange("(g p j) -> p g j", g=PASSES, j=PACK))
+        load_values(2)
+        load_values(3)
         make_identity(nc, ident[:])
+        nc.gpsimd.memset(minus_one[:], -1.0)
+        nc.vector.memset(placed[:], 0.0)
 
         q_bf = sb.tile([P, Q, PACK], BF16, name="q_bf", align_bytes=64)
         q_codes = sb.tile([P, Q], U32, name="q_codes", align_bytes=64)
@@ -78,9 +90,6 @@ def tile_attend_mqa_ownlists_kernel(tc, query, keys_words, keys_scales, fac, val
         nc.vector.quantize_mx(
             out=q_codes[:].bitcast(FP8X4), scales=q_scales[:], in_=q_bf[:].rearrange("p q j -> p (q j)")
         )
-
-        placed = sb.tile([P, T], F32, name="placed", tag="q_raw")
-        nc.vector.memset(placed[:], 0.0)
 
         scores = sb.tile([P, T], F32, name="scores")
         start = 0
@@ -98,7 +107,7 @@ def tile_attend_mqa_ownlists_kernel(tc, query, keys_words, keys_scales, fac, val
                 start=True,
                 stop=True,
             )
-            if n % 2 == 0:
+            if n in SCALAR_BANKS:
                 nc.scalar.copy(out=scores[:, cols], in_=bank[:])
             else:
                 nc.vector.tensor_copy(out=scores[:, cols], in_=bank[:])
@@ -110,22 +119,39 @@ def tile_attend_mqa_ownlists_kernel(tc, query, keys_words, keys_scales, fac, val
         nc.vector.tensor_reduce(out=neg_max[:], in_=picked[:], axis=AXIS_X, op=ALU.max, negate=True)
 
         p_first = sb.tile([P, FIRST], F32, name="p_first")
-        p_rest = sb.tile([P, SLOTS - FIRST], F32, name="p_rest")
-        sum_first = sb.tile([P, 1], F32, name="sum_first")
-        sum_rest = sb.tile([P, 1], F32, name="sum_rest")
+        p_all = sb.tile([P, SLOTS], F32, name="p_all")
         total = sb.tile([P, 1], F32, name="total")
-        inv_total = sb.tile([P, 1], F32, name="inv_total", tag="inv_total", align_bytes=64)
-        nc.scalar.activation(
-            out=p_first[:], in_=picked[:, :FIRST], func=ACT.Exp, bias=neg_max[:], accum_out=sum_first[:]
-        )
-        nc.scalar.activation(
-            out=p_rest[:], in_=picked[:, FIRST:], func=ACT.Exp, bias=neg_max[:], accum_out=sum_rest[:]
-        )
-        nc.scalar.activation(out=total[:], in_=sum_first[:], func=ACT.Identity, bias=sum_rest[:])
+        inv_total = sb.tile([P, 1], F32, name="inv_total")
+        nc.scalar.activation(out=p_first[:], in_=picked[:, :FIRST], func=ACT.Exp, bias=neg_max[:])
+        nc.scalar.activation(out=p_all[:], in_=picked[:], func=ACT.Exp, bias=neg_max[:], accum_out=total[:])
+        nc.gpsimd.tensor_tensor(out=inv_total[:], in0=total[:], in1=minus_one[:], op=ALU.pow)
 
-        nc.vector.tensor_copy(placed[:].indirect(offsets[:, 0:8]), p_first[:])
-        nc.vector.tensor_copy(placed[:].indirect(offsets[:, 8:32]), p_rest[:])
-        nc.vector.reciprocal(out=inv_total[:], in_=total[:])
+        nc.vector.tensor_copy(placed[:].indirect(offsets[:, : FIRST // 16]), p_first[:])
+        nc.vector.tensor_copy(placed[:].indirect(offsets[:, FIRST // 16 :]), p_all[:, FIRST:])
+
+        early_bf = sb.tile([P, EARLY_UNITS, OUT_WIDTH, PACK], BF16, name="early_bf", align_bytes=64)
+        late_bf = sb.tile([P, UNITS - EARLY_UNITS, OUT_WIDTH, PACK], BF16, name="late_bf", tag="picked", align_bytes=64)
+        v_bf = [early_bf[:, i] if i < EARLY_UNITS else late_bf[:, i - EARLY_UNITS] for i in range(UNITS)]
+        v_codes = sb.tile([P, UNITS * OUT_WIDTH], U32, name="v_codes", align_bytes=64)
+        unit_codes = [v_codes[:, i * OUT_WIDTH : (i + 1) * OUT_WIDTH] for i in range(UNITS)]
+        unit_scales = {}
+        for i in range(UNITS):
+            in_half = (i % 2) * OUT_WIDTH
+            nc.scalar.copy(
+                out=v_bf[i].rearrange("p (c i) j -> p c j i", i=4),
+                in_=v_raw[i // 2][:, :, in_half : in_half + OUT_WIDTH].rearrange("p j (c i) -> p c j i", i=4),
+            )
+
+        def quantize_units(first, count, scales):
+            for n in range(count):
+                i = first + n
+                unit_scales[i] = scales[:, n * OUT_WIDTH : (n + 1) * OUT_WIDTH]
+                nc.vector.quantize_mx(
+                    out=unit_codes[i].bitcast(FP8X4), scales=unit_scales[i], in_=v_bf[i].rearrange("p e j -> p (e j)")
+                )
+
+        pass0_scales = sb.tile([P, 4 * OUT_WIDTH], U8, name="pass0_scales", align_bytes=64)
+        quantize_units(0, 4, pass0_scales)
 
         fac_rows = []
         for g in range(PASSES):
@@ -140,7 +166,7 @@ def tile_attend_mqa_ownlists_kernel(tc, query, keys_words, keys_scales, fac, val
             turned_g = ps.tile([P, 2, Q], F32, name="turned%d" % g, tag="bank%d" % (2 + g))
             fac_v = fac_rows[g][:].rearrange("q (u e) p -> q u p e", e=2)
             for u in range(2):
-                w_pairs = sb.tile([P, P, 2], BF16, name="w_pairs%d%d" % (g, u))
+                w_pairs = sb.tile([P, P, 2], BF16, name="w_pairs%d%d" % (g, u), tag="w_pairs%d%d" % (g, u), align_bytes=64)
                 nc.vector.scalar_tensor_tensor(
                     out=w_pairs[:],
                     in0=placed_v[:, g, u],
@@ -154,50 +180,25 @@ def tile_attend_mqa_ownlists_kernel(tc, query, keys_words, keys_scales, fac, val
                 )
             turned.append(turned_g)
 
-        units = [(g, n) for g in range(PASSES) for n in range(4)]
-        v_codes = sb.tile([P, len(units) * OUT_WIDTH], U32, name="v_codes", align_bytes=64)
-        early_scales = sb.tile([P, EARLY_UNITS * OUT_WIDTH], U8, name="early_scales", align_bytes=64)
-        late_scales = sb.tile(
-            [P, (len(units) - EARLY_UNITS) * OUT_WIDTH], U8, name="late_scales", tag="inv_total", align_bytes=64
-        )
-        unit_codes = {}
-        unit_scales = {}
-        for i, (g, n) in enumerate(units):
-            h, in_half = divmod(n * OUT_WIDTH, HALF_E)
-            if i % 2 == 0:
-                bf_tag = "picked" if i == EARLY_UNITS else "v_bf%d" % i
-                v_pair = sb.tile([P, 2, OUT_WIDTH, PACK], BF16, name="v_bf%d" % i, tag=bf_tag, align_bytes=64)
-            v_bf = v_pair[:, i % 2]
-            nc.scalar.copy(
-                out=v_bf.rearrange("p (c i) j -> p c j i", i=4),
-                in_=v_raw[g, h][:, :, in_half : in_half + OUT_WIDTH].rearrange("p j (c i) -> p c j i", i=4),
-            )
-            unit_codes[g, n] = v_codes[:, i * OUT_WIDTH : (i + 1) * OUT_WIDTH]
-            if i < EARLY_UNITS:
-                unit_scales[g, n] = early_scales[:, i * OUT_WIDTH : (i + 1) * OUT_WIDTH]
-            else:
-                late = i - EARLY_UNITS
-                unit_scales[g, n] = late_scales[:, late * OUT_WIDTH : (late + 1) * OUT_WIDTH]
-            nc.vector.quantize_mx(
-                out=unit_codes[g, n].bitcast(FP8X4),
-                scales=unit_scales[g, n],
-                in_=v_bf.rearrange("p e j -> p (e j)"),
-            )
+        mid_scales = sb.tile([P, 3 * OUT_WIDTH], U8, name="mid_scales", tag="w_pairs01", align_bytes=64)
+        quantize_units(4, 3, mid_scales)
 
         w_codes = []
         w_scales = []
         for g in range(PASSES):
-            bf_tag = "v_raw11" if g == 0 else "w_bf1"
-            w_bf = sb.tile([P, Q * PACK], BF16, name="w_bf%d" % g, tag=bf_tag, align_bytes=64)
+            w_bf = tail.tile([P, Q * PACK], BF16, name="w_bf%d" % g, offset=g * Q * PACK * 2, align_bytes=64)
             nc.scalar.copy(
                 out=w_bf[:].bitcast(F32).rearrange("p (q u) -> p q u", u=2),
                 in_=turned[g][:].rearrange("p u q -> p q u"),
             )
-            codes_g = sb.tile([P, Q], U32, name="w_codes%d" % g, tag="v_bf6" if g == 0 else "w_codes1", align_bytes=64)
+            codes_g = sb.tile([P, Q], U32, name="w_codes%d" % g, align_bytes=64)
             scales_g = sb.tile([P, Q], U8, name="w_scales%d" % g, align_bytes=64)
             nc.vector.quantize_mx(out=codes_g[:].bitcast(FP8X4), scales=scales_g[:], in_=w_bf[:])
             w_codes.append(codes_g)
             w_scales.append(scales_g)
+            if g == 0:
+                last_scales = tail.tile([P, OUT_WIDTH], U8, name="last_scales", offset=0, align_bytes=64)
+                quantize_units(7, 1, last_scales)
 
         acc = [ps.tile([P, OUT_WIDTH], F32, name="acc%d" % n, tag="bank%d" % (4 + n)) for n in range(4)]
         for g in range(PASSES):
@@ -206,8 +207,8 @@ def tile_attend_mqa_ownlists_kernel(tc, query, keys_words, keys_scales, fac, val
                     out=acc[n][:],
                     lhsT=w_codes[g][:].bitcast(FP8X4),
                     lhsT_scale=w_scales[g][:],
-                    rhs=unit_codes[g, n].bitcast(FP8X4),
-                    rhs_scale=unit_scales[g, n],
+                    rhs=unit_codes[4 * g + n].bitcast(FP8X4),
+                    rhs_scale=unit_scales[4 * g + n],
                     start=(g == 0),
                     stop=(g == PASSES - 1),
                 )

@@ -30,6 +30,7 @@ SCALAR_BANKS = (0, 2)
 OUT_WIDTH = 128
 UNITS = PASSES * E // OUT_WIDTH
 EARLY_UNITS = 3
+POOL_WORDS = 48
 
 
 def tile_attend_mqa_ownlists_kernel(tc, query, keys_words, keys_scales, fac, vals, offs, out):
@@ -154,11 +155,20 @@ def tile_attend_mqa_ownlists_kernel(tc, query, keys_words, keys_scales, fac, val
         quantize_units(0, 4, pass0_scales)
 
         fac_rows = []
+        factors = []
         for g in range(PASSES):
             rows_g = ps.tile([P, PACK, P], F32, name="fac_rows%d" % g, tag="bank%d" % g)
             for j in range(PACK):
                 nc.tensor.transpose(rows_g[:, j, :], fac_cols[:, g, j : j + 1].to_broadcast([P, P]), ident[:])
             fac_rows.append(rows_g)
+            factors_g = sb.tile([P, POOL_WORDS, 2], F32, name="factors%d" % g)
+            nc.scalar.activation(
+                out=factors_g[:],
+                in_=rows_g[:, 2:, P - POOL_WORDS :].rearrange("q e p -> q p e"),
+                func=ACT.Copy,
+                scale=inv_total[:],
+            )
+            factors.append(factors_g)
 
         placed_v = placed[:].rearrange("q (g p u e) -> q g u p e", g=PASSES, u=2, e=2)
         turned = []
@@ -167,11 +177,16 @@ def tile_attend_mqa_ownlists_kernel(tc, query, keys_words, keys_scales, fac, val
             fac_v = fac_rows[g][:].rearrange("q (u e) p -> q u p e", e=2)
             for u in range(2):
                 w_pairs = sb.tile([P, P, 2], BF16, name="w_pairs%d%d" % (g, u), tag="w_pairs%d%d" % (g, u), align_bytes=64)
+                split = P - POOL_WORDS if u == 1 else P
+                if split < P:
+                    nc.gpsimd.tensor_tensor(
+                        out=w_pairs[:, split:], in0=placed_v[:, g, u, split:], in1=factors[g][:], op=ALU.mult
+                    )
                 nc.vector.scalar_tensor_tensor(
-                    out=w_pairs[:],
-                    in0=placed_v[:, g, u],
+                    out=w_pairs[:, :split],
+                    in0=placed_v[:, g, u, :split],
                     scalar=inv_total[:],
-                    in1=fac_v[:, u],
+                    in1=fac_v[:, u, :split],
                     op0=ALU.mult,
                     op1=ALU.mult,
                 )

@@ -46,7 +46,6 @@ def tile_attend_mqa_ownlists_kernel(tc, query, keys_words, keys_scales, fac, val
         k_scales = sb.tile([P, QUARTER], U8, name="k_scales", align_bytes=64)
         fac_cols = sb.tile([P, PASSES, PACK], F32, name="fac_cols")
         ident = sb.tile([P, P], F32, name="ident")
-        minus_one = sb.tile([P, 1], F32, name="minus_one")
         placed = sb.tile([P, T], F32, name="placed")
         v_raw = [sb.tile([P, PACK, HALF_E], F32, name="v_raw%d" % n) for n in range(3)]
         v_raw.append(tail.tile([P, PACK, HALF_E], F32, name="v_raw3", offset=0, align_bytes=64))
@@ -73,9 +72,9 @@ def tile_attend_mqa_ownlists_kernel(tc, query, keys_words, keys_scales, fac, val
         nc.sync.dma_start(out=fac_cols[:], in_=fac[0].rearrange("(g p j) -> p g j", g=PASSES, j=PACK))
         load_values(2)
         load_values(3)
-        make_identity(nc, ident[:])
-        nc.gpsimd.memset(minus_one[:], -1.0)
         nc.vector.memset(placed[:], 0.0)
+        nc.vector.memset(ident[:], 0.0)
+        make_identity(nc, ident[:], nomemset=True)
 
         q_bf = sb.tile([P, Q, PACK], BF16, name="q_bf", align_bytes=64)
         q_codes = sb.tile([P, Q], U32, name="q_codes", align_bytes=64)
@@ -125,9 +124,8 @@ def tile_attend_mqa_ownlists_kernel(tc, query, keys_words, keys_scales, fac, val
         inv_total = sb.tile([P, 1], F32, name="inv_total")
         nc.scalar.activation(out=p_first[:], in_=picked[:, :FIRST], func=ACT.Exp, bias=neg_max[:])
         nc.scalar.activation(out=p_all[:], in_=picked[:], func=ACT.Exp, bias=neg_max[:], accum_out=total[:])
-        nc.gpsimd.tensor_tensor(out=inv_total[:], in0=total[:], in1=minus_one[:], op=ALU.pow)
-
         nc.vector.tensor_copy(placed[:].indirect(offsets[:, : FIRST // 16]), p_first[:])
+        nc.vector.reciprocal(out=inv_total[:], in_=total[:])
         nc.vector.tensor_copy(placed[:].indirect(offsets[:, FIRST // 16 :]), p_all[:, FIRST:])
 
         early_bf = sb.tile([P, EARLY_UNITS, OUT_WIDTH, PACK], BF16, name="early_bf", align_bytes=64)

@@ -21,38 +21,39 @@ P = 128
 PACK = 4
 K_PASS = P * PACK
 PASSES = T // K_PASS
+LIST_ROWS = 16
 QUARTER = T // 4
-HALF_E = E // 2
-FIRST = 128
+UNIT = 128
+UNITS_PER_PASS = E // UNIT
+UNITS = PASSES * UNITS_PER_PASS
+HEAD_SLOTS = 160
+HEADROOM = 32.0
 Q_VECTOR = 88
 SCORE_WIDTHS = (256, 256, 128, 128, 128, 128)
 SCALAR_BANKS = (0, 2)
-OUT_WIDTH = 128
-UNITS = PASSES * E // OUT_WIDTH
-EARLY_UNITS = 3
-POOL_WORDS = 48
+EARLY_UNITS = 2
+CASTS_BEFORE_FACTORS = 5
+POOL_WORDS = (64, 32)
 
 
 def tile_attend_mqa_ownlists_kernel(tc, query, keys_words, keys_scales, fac, vals, offs, out):
     nc = tc.nc
     with ExitStack() as ctx:
         sb = ctx.enter_context(tc.tile_pool(name="sb", bufs=1))
-        tail = ctx.enter_context(tc.tile_pool(name="tail", bufs=1))
         ps = ctx.enter_context(tc.psum_pool(name="ps", bufs=1))
 
-        offsets = sb.tile([P, SLOTS // 16], U16, name="offsets")
+        offsets = sb.tile([P, SLOTS // LIST_ROWS], U16, name="offsets")
         q_raw = sb.tile([P, PACK, Q], F32, name="q_raw")
         k_words = [sb.tile([P, T // 2], U32, name="k_words%d" % h, align_bytes=64) for h in range(2)]
         k_scales = sb.tile([P, QUARTER], U8, name="k_scales", align_bytes=64)
         fac_cols = sb.tile([P, PASSES, PACK], F32, name="fac_cols")
+        v_raw = [sb.tile([P, PACK, 2 * UNIT], F32, name="v_raw%d" % n) for n in range(UNITS // 2)]
         ident = sb.tile([P, P], F32, name="ident")
         placed = sb.tile([P, T], F32, name="placed")
-        v_raw = [sb.tile([P, PACK, HALF_E], F32, name="v_raw%d" % n) for n in range(3)]
-        v_raw.append(tail.tile([P, PACK, HALF_E], F32, name="v_raw3", offset=0, align_bytes=64))
 
         def load_values(n):
             g, h = divmod(n, 2)
-            rows = vals[g * K_PASS : (g + 1) * K_PASS, h * HALF_E : (h + 1) * HALF_E]
+            rows = vals[g * K_PASS : (g + 1) * K_PASS, h * 2 * UNIT : (h + 1) * 2 * UNIT]
             nc.sync.dma_start(out=v_raw[n][:], in_=rows.rearrange("(p j) e -> p j e", j=PACK))
 
         nc.vector.memset(k_scales[:].bitcast(I32), 0)
@@ -91,7 +92,7 @@ def tile_attend_mqa_ownlists_kernel(tc, query, keys_words, keys_scales, fac, val
             out=q_codes[:].bitcast(FP8X4), scales=q_scales[:], in_=q_bf[:].rearrange("p q j -> p (q j)")
         )
 
-        scores = sb.tile([P, T], F32, name="scores")
+        scores = sb.tile([P, T], F32, name="scores", tag="scores", align_bytes=64)
         start = 0
         for n, width in enumerate(SCORE_WIDTHS):
             cols = slice(start, start + width)
@@ -113,44 +114,72 @@ def tile_attend_mqa_ownlists_kernel(tc, query, keys_words, keys_scales, fac, val
                 nc.vector.tensor_copy(out=scores[:, cols], in_=bank[:])
             start = start + width
 
-        picked = sb.tile([P, SLOTS], F32, name="picked", tag="picked", align_bytes=64)
-        nc.vector.tensor_copy(picked[:], scores[:].indirect(offsets[:]))
-        neg_max = sb.tile([P, 1], F32, name="neg_max")
-        nc.vector.tensor_reduce(out=neg_max[:], in_=picked[:], axis=AXIS_X, op=ALU.max, negate=True)
-
-        p_first = sb.tile([P, FIRST], F32, name="p_first")
-        p_all = sb.tile([P, SLOTS], F32, name="p_all")
-        total = sb.tile([P, 1], F32, name="total")
-        inv_total = sb.tile([P, 1], F32, name="inv_total")
-        nc.scalar.activation(out=p_first[:], in_=picked[:, :FIRST], func=ACT.Exp, bias=neg_max[:])
-        nc.scalar.activation(out=p_all[:], in_=picked[:], func=ACT.Exp, bias=neg_max[:], accum_out=total[:])
-        nc.vector.tensor_copy(placed[:].indirect(offsets[:, : FIRST // 16]), p_first[:])
-        nc.vector.reciprocal(out=inv_total[:], in_=total[:])
-        nc.vector.tensor_copy(placed[:].indirect(offsets[:, FIRST // 16 :]), p_all[:, FIRST:])
-
-        early_bf = sb.tile([P, EARLY_UNITS, OUT_WIDTH, PACK], BF16, name="early_bf", align_bytes=64)
-        late_bf = sb.tile([P, UNITS - EARLY_UNITS, OUT_WIDTH, PACK], BF16, name="late_bf", tag="picked", align_bytes=64)
-        v_bf = [early_bf[:, i] if i < EARLY_UNITS else late_bf[:, i - EARLY_UNITS] for i in range(UNITS)]
-        v_codes = sb.tile([P, UNITS * OUT_WIDTH], U32, name="v_codes", align_bytes=64)
-        unit_codes = [v_codes[:, i * OUT_WIDTH : (i + 1) * OUT_WIDTH] for i in range(UNITS)]
-        unit_scales = {}
-        for i in range(UNITS):
-            in_half = (i % 2) * OUT_WIDTH
-            nc.scalar.copy(
-                out=v_bf[i].rearrange("p (c i) j -> p c j i", i=4),
-                in_=v_raw[i // 2][:, :, in_half : in_half + OUT_WIDTH].rearrange("p j (c i) -> p c j i", i=4),
+        head_offsets = offsets[:, : HEAD_SLOTS // LIST_ROWS]
+        rest_offsets = offsets[:, HEAD_SLOTS // LIST_ROWS :]
+        negated = sb.tile([P, SLOTS], F32, name="negated", tag="negated", align_bytes=64)
+        for first in (0, SLOTS // 2):
+            nc.vector.tensor_scalar(
+                out=negated[:, first : first + SLOTS // 2],
+                in0=scores[:].indirect(offsets[:, first // LIST_ROWS : (first + SLOTS // 2) // LIST_ROWS]),
+                scalar1=-1.0,
+                scalar2=0.0,
+                op0=ALU.mult,
+                op1=ALU.add,
             )
+        head_shift = sb.tile([P, 1], F32, name="head_shift", tag="head_shift", align_bytes=64)
+        nc.vector.tensor_reduce(out=head_shift[:], in_=negated[:, :HEAD_SLOTS], axis=AXIS_X, op=ALU.min)
+        raised = sb.tile([P, SLOTS - HEAD_SLOTS], F32, name="raised")
+        rest_shift = sb.tile([P, 1], F32, name="rest_shift")
+        nc.vector.tensor_scalar(
+            out=raised[:],
+            in0=negated[:, HEAD_SLOTS:],
+            scalar1=HEADROOM,
+            scalar2=head_shift[:],
+            op0=ALU.add,
+            op1=ALU.min,
+            accum_out=rest_shift[:],
+        )
 
-        def quantize_units(first, count, scales):
-            for n in range(count):
-                i = first + n
-                unit_scales[i] = scales[:, n * OUT_WIDTH : (n + 1) * OUT_WIDTH]
-                nc.vector.quantize_mx(
-                    out=unit_codes[i].bitcast(FP8X4), scales=unit_scales[i], in_=v_bf[i].rearrange("p e j -> p (e j)")
+        p_head = sb.tile([P, HEAD_SLOTS], F32, name="p_head")
+        p_all = sb.tile([P, SLOTS], F32, name="p_all")
+        total = sb.tile([P, 1], F32, name="total", tag="total", align_bytes=64)
+        inv_total = sb.tile([P, 1], F32, name="inv_total")
+        nc.scalar.activation(out=p_head[:], in_=negated[:, :HEAD_SLOTS], func=ACT.Exp, bias=head_shift[:], scale=-1.0)
+        nc.scalar.activation(
+            out=p_all[:], in_=negated[:], func=ACT.Exp, bias=rest_shift[:], scale=-1.0, accum_out=total[:]
+        )
+        nc.vector.tensor_copy(placed[:].indirect(head_offsets), p_head[:])
+        nc.vector.reciprocal(out=inv_total[:], in_=total[:])
+        nc.vector.tensor_copy(placed[:].indirect(rest_offsets), p_all[:, HEAD_SLOTS:])
+
+        early_bf = sb.tile([P, EARLY_UNITS, UNIT, PACK], BF16, name="early_bf", align_bytes=64)
+        late_bf = sb.tile([P, UNITS - EARLY_UNITS, UNIT, PACK], BF16, name="late_bf", tag="negated", align_bytes=64)
+        v_bf = [early_bf[:, i] if i < EARLY_UNITS else late_bf[:, i - EARLY_UNITS] for i in range(UNITS)]
+        v_codes = sb.tile([P, UNITS * UNIT], U32, name="v_codes", align_bytes=64)
+        v_scales = {}
+
+        def cast_units(first, stop):
+            for i in range(first, stop):
+                cols = slice((i % 2) * UNIT, (i % 2 + 1) * UNIT)
+                nc.scalar.copy(
+                    out=v_bf[i].rearrange("p (c i) j -> p c j i", i=4),
+                    in_=v_raw[i // 2][:, :, cols].rearrange("p j (c i) -> p c j i", i=4),
                 )
 
-        pass0_scales = sb.tile([P, 4 * OUT_WIDTH], U8, name="pass0_scales", align_bytes=64)
-        quantize_units(0, 4, pass0_scales)
+        def quantize_units(first, stop, tag):
+            scales = sb.tile([P, (stop - first) * UNIT], U8, name="v_scales%d" % first, tag=tag, align_bytes=64)
+            for i in range(first, stop):
+                v_scales[i] = scales[:, (i - first) * UNIT : (i - first + 1) * UNIT]
+                nc.vector.quantize_mx(
+                    out=v_codes[:, i * UNIT : (i + 1) * UNIT].bitcast(FP8X4),
+                    scales=v_scales[i],
+                    in_=v_bf[i].rearrange("p e j -> p (e j)"),
+                )
+
+        cast_units(0, CASTS_BEFORE_FACTORS)
+        quantize_units(0, 1, "scores")
+        quantize_units(1, 2, "head_shift")
+        quantize_units(2, 3, "total")
 
         fac_rows = []
         factors = []
@@ -158,33 +187,30 @@ def tile_attend_mqa_ownlists_kernel(tc, query, keys_words, keys_scales, fac, val
             rows_g = ps.tile([P, PACK, P], F32, name="fac_rows%d" % g, tag="bank%d" % g)
             for j in range(PACK):
                 nc.tensor.transpose(rows_g[:, j, :], fac_cols[:, g, j : j + 1].to_broadcast([P, P]), ident[:])
-            fac_rows.append(rows_g)
-            factors_g = sb.tile([P, POOL_WORDS, 2], F32, name="factors%d" % g)
+            fac_rows.append(rows_g[:].rearrange("q (u e) p -> q u p e", e=2))
+            factors.append(sb.tile([P, POOL_WORDS[g], 2], F32, name="factors%d" % g))
             nc.scalar.activation(
-                out=factors_g[:],
-                in_=rows_g[:, 2:, P - POOL_WORDS :].rearrange("q e p -> q p e"),
-                func=ACT.Copy,
-                scale=inv_total[:],
+                out=factors[g][:], in_=fac_rows[g][:, 1, P - POOL_WORDS[g] :], func=ACT.Copy, scale=inv_total[:]
             )
-            factors.append(factors_g)
+        cast_units(CASTS_BEFORE_FACTORS, UNITS)
 
         placed_v = placed[:].rearrange("q (g p u e) -> q g u p e", g=PASSES, u=2, e=2)
         turned = []
         for g in range(PASSES):
             turned_g = ps.tile([P, 2, Q], F32, name="turned%d" % g, tag="bank%d" % (2 + g))
-            fac_v = fac_rows[g][:].rearrange("q (u e) p -> q u p e", e=2)
             for u in range(2):
-                w_pairs = sb.tile([P, P, 2], BF16, name="w_pairs%d%d" % (g, u), tag="w_pairs%d%d" % (g, u), align_bytes=64)
-                split = P - POOL_WORDS if u == 1 else P
-                if split < P:
+                name = "w_pairs%d%d" % (g, u)
+                w_pairs = sb.tile([P, P, 2], BF16, name=name, tag=name, align_bytes=64)
+                words = P - POOL_WORDS[g] if u == 1 else P
+                if u == 1:
                     nc.gpsimd.tensor_tensor(
-                        out=w_pairs[:, split:], in0=placed_v[:, g, u, split:], in1=factors[g][:], op=ALU.mult
+                        out=w_pairs[:, words:], in0=placed_v[:, g, u, words:], in1=factors[g][:], op=ALU.mult
                     )
                 nc.vector.scalar_tensor_tensor(
-                    out=w_pairs[:, :split],
-                    in0=placed_v[:, g, u, :split],
+                    out=w_pairs[:, :words],
+                    in0=placed_v[:, g, u, :words],
                     scalar=inv_total[:],
-                    in1=fac_v[:, u, :split],
+                    in1=fac_rows[g][:, u, :words],
                     op0=ALU.mult,
                     op1=ALU.mult,
                 )
@@ -193,13 +219,10 @@ def tile_attend_mqa_ownlists_kernel(tc, query, keys_words, keys_scales, fac, val
                 )
             turned.append(turned_g)
 
-        mid_scales = sb.tile([P, 3 * OUT_WIDTH], U8, name="mid_scales", tag="w_pairs01", align_bytes=64)
-        quantize_units(4, 3, mid_scales)
-
         w_codes = []
         w_scales = []
         for g in range(PASSES):
-            w_bf = tail.tile([P, Q * PACK], BF16, name="w_bf%d" % g, offset=g * Q * PACK * 2, align_bytes=64)
+            w_bf = sb.tile([P, Q * PACK], BF16, name="w_bf%d" % g, tag="w_bf%d" % g, align_bytes=64)
             nc.scalar.copy(
                 out=w_bf[:].bitcast(F32).rearrange("p (q u) -> p q u", u=2),
                 in_=turned[g][:].rearrange("p u q -> p q u"),
@@ -209,24 +232,24 @@ def tile_attend_mqa_ownlists_kernel(tc, query, keys_words, keys_scales, fac, val
             nc.vector.quantize_mx(out=codes_g[:].bitcast(FP8X4), scales=scales_g[:], in_=w_bf[:])
             w_codes.append(codes_g)
             w_scales.append(scales_g)
-            if g == 0:
-                last_scales = tail.tile([P, OUT_WIDTH], U8, name="last_scales", offset=0, align_bytes=64)
-                quantize_units(7, 1, last_scales)
+        quantize_units(3, UNITS - 1, "w_pairs00")
+        quantize_units(UNITS - 1, UNITS, "w_bf0")
 
-        acc = [ps.tile([P, OUT_WIDTH], F32, name="acc%d" % n, tag="bank%d" % (4 + n)) for n in range(4)]
+        acc = [ps.tile([P, UNIT], F32, name="acc%d" % n, tag="bank%d" % (4 + n)) for n in range(UNITS_PER_PASS)]
         for g in range(PASSES):
-            for n in range(4):
+            for n in range(UNITS_PER_PASS):
+                i = g * UNITS_PER_PASS + n
                 nc.tensor.matmul_mx(
                     out=acc[n][:],
                     lhsT=w_codes[g][:].bitcast(FP8X4),
                     lhsT_scale=w_scales[g][:],
-                    rhs=unit_codes[4 * g + n].bitcast(FP8X4),
-                    rhs_scale=unit_scales[4 * g + n],
+                    rhs=v_codes[:, i * UNIT : (i + 1) * UNIT].bitcast(FP8X4),
+                    rhs_scale=v_scales[i],
                     start=(g == 0),
                     stop=(g == PASSES - 1),
                 )
         for h in range(2):
-            result = sb.tile([P, HALF_E], F32, name="result%d" % h)
-            nc.scalar.copy(out=result[:, :OUT_WIDTH], in_=acc[2 * h][:])
-            nc.vector.tensor_copy(out=result[:, OUT_WIDTH:], in_=acc[2 * h + 1][:])
-            nc.sync.dma_start(out=out[:, h * HALF_E : (h + 1) * HALF_E], in_=result[:])
+            result = sb.tile([P, 2 * UNIT], F32, name="result%d" % h)
+            nc.scalar.copy(out=result[:, :UNIT], in_=acc[2 * h][:])
+            nc.vector.tensor_copy(out=result[:, UNIT:], in_=acc[2 * h + 1][:])
+            nc.sync.dma_start(out=out[:, h * 2 * UNIT : (h + 1) * 2 * UNIT], in_=result[:])

@@ -29,8 +29,10 @@ UNITS = PASSES * UNITS_PER_PASS
 HEAD_SLOTS = 160
 HEADROOM = 32.0
 Q_VECTOR = 88
-SCORE_WIDTHS = (256, 256, 128, 128, 128, 128)
-SCALAR_BANKS = (0, 2)
+FIRST_KEYS = 384
+SCORE_WIDTHS = (256, 128, 128, 256, 128, 128)
+SCALAR_BANKS = (0, 3)
+STORES = ((0, 1), (1, 2), (2, 4))
 EARLY_UNITS = 2
 CASTS_BEFORE_FACTORS = 5
 POOL_WORDS = (64, 32)
@@ -44,7 +46,8 @@ def tile_attend_mqa_ownlists_kernel(tc, query, keys_words, keys_scales, fac, val
 
         offsets = sb.tile([P, SLOTS // LIST_ROWS], U16, name="offsets")
         q_raw = sb.tile([P, PACK, Q], F32, name="q_raw")
-        k_words = [sb.tile([P, T // 2], U32, name="k_words%d" % h, align_bytes=64) for h in range(2)]
+        key_cuts = ((0, FIRST_KEYS), (FIRST_KEYS, T))
+        k_words = [sb.tile([P, b - a], U32, name="k_words%d" % a, align_bytes=64) for a, b in key_cuts]
         k_scales = sb.tile([P, QUARTER], U8, name="k_scales", align_bytes=64)
         fac_cols = sb.tile([P, PASSES, PACK], F32, name="fac_cols")
         v_raw = [sb.tile([P, PACK, 2 * UNIT], F32, name="v_raw%d" % n) for n in range(UNITS // 2)]
@@ -59,14 +62,14 @@ def tile_attend_mqa_ownlists_kernel(tc, query, keys_words, keys_scales, fac, val
         nc.vector.memset(k_scales[:].bitcast(I32), 0)
         nc.sync.dma_start(out=q_raw[:], in_=query.rearrange("(p j) q -> p j q", j=PACK))
         key_ints = keys_words[0].rearrange("p n t -> p (n t)").bitcast(I32)
-        nc.sync.dma_start(out=k_words[0][:].bitcast(I32), in_=key_ints[:, : T // 2])
+        nc.sync.dma_start(out=k_words[0][:].bitcast(I32), in_=key_ints[:, :FIRST_KEYS])
         scale_words = keys_scales[0].bitcast(I32)
         for quad in range(4):
             nc.sync.dma_start(
                 out=k_scales[32 * quad : 32 * quad + 16, :].bitcast(I32),
                 in_=scale_words[4 * quad : 4 * quad + 4, :].rearrange("r (h c) -> h r c", h=4),
             )
-        nc.sync.dma_start(out=k_words[1][:].bitcast(I32), in_=key_ints[:, T // 2 :])
+        nc.sync.dma_start(out=k_words[1][:].bitcast(I32), in_=key_ints[:, FIRST_KEYS:])
         load_values(0)
         nc.sync.dma_start(offsets[:], offs)
         load_values(1)
@@ -97,13 +100,14 @@ def tile_attend_mqa_ownlists_kernel(tc, query, keys_words, keys_scales, fac, val
         for n, width in enumerate(SCORE_WIDTHS):
             cols = slice(start, start + width)
             quarter, in_quarter = divmod(start, QUARTER)
-            half, in_half = divmod(start, T // 2)
+            piece = 0 if start < FIRST_KEYS else 1
+            in_piece = start - key_cuts[piece][0]
             bank = ps.tile([P, width], F32, name="score_bank%d" % n, tag="bank%d" % n)
             nc.tensor.matmul_mx(
                 out=bank[:],
                 lhsT=q_codes[:].bitcast(FP8X4),
                 lhsT_scale=q_scales[:],
-                rhs=k_words[half][:, in_half : in_half + width].bitcast(FP8X4),
+                rhs=k_words[piece][:, in_piece : in_piece + width].bitcast(FP8X4),
                 rhs_scale=k_scales[4 * quarter : P, in_quarter : in_quarter + width],
                 start=True,
                 stop=True,
@@ -248,8 +252,9 @@ def tile_attend_mqa_ownlists_kernel(tc, query, keys_words, keys_scales, fac, val
                     start=(g == 0),
                     stop=(g == PASSES - 1),
                 )
-        for h in range(2):
-            result = sb.tile([P, 2 * UNIT], F32, name="result%d" % h)
-            nc.scalar.copy(out=result[:, :UNIT], in_=acc[2 * h][:])
-            nc.vector.tensor_copy(out=result[:, UNIT:], in_=acc[2 * h + 1][:])
-            nc.sync.dma_start(out=out[:, h * 2 * UNIT : (h + 1) * 2 * UNIT], in_=result[:])
+        for first, stop in STORES:
+            result = sb.tile([P, (stop - first) * UNIT], F32, name="result%d" % first)
+            copy = nc.scalar.copy if first < UNITS_PER_PASS // 2 else nc.vector.tensor_copy
+            for n in range(first, stop):
+                copy(out=result[:, (n - first) * UNIT : (n - first + 1) * UNIT], in_=acc[n][:])
+            nc.sync.dma_start(out=out[:, first * UNIT : stop * UNIT], in_=result[:])

@@ -30,8 +30,8 @@ HEAD_SLOTS = 160
 HEADROOM = 32.0
 Q_VECTOR = 88
 FIRST_KEYS = 384
-SCORE_WIDTHS = (256, 128, 128, 256, 128, 128)
-SCALAR_BANKS = (0, 3)
+SCORE_WIDTHS = (256, 128, 128, 128, 128, 128, 128)
+SCALAR_BANKS = (0, 3, 5)
 STORES = ((0, 1), (1, 2), (2, 4))
 EARLY_UNITS = 2
 CASTS_BEFORE_FACTORS = 5
@@ -236,8 +236,9 @@ def tile_attend_mqa_ownlists_kernel(tc, query, keys_words, keys_scales, fac, val
             nc.vector.quantize_mx(out=codes_g[:].bitcast(FP8X4), scales=scales_g[:], in_=w_bf[:])
             w_codes.append(codes_g)
             w_scales.append(scales_g)
-        quantize_units(3, UNITS - 1, "w_pairs00")
-        quantize_units(UNITS - 1, UNITS, "w_bf0")
+        quantize_units(3, UNITS - 2, "w_pairs00")
+        quantize_units(UNITS - 2, UNITS - 1, "w_bf0")
+        quantize_units(UNITS - 1, UNITS, "w_bf1")
 
         acc = [ps.tile([P, UNIT], F32, name="acc%d" % n, tag="bank%d" % (4 + n)) for n in range(UNITS_PER_PASS)]
         for g in range(PASSES):

@@ -32,10 +32,10 @@ Q_VECTOR = 88
 FIRST_KEYS = 384
 SCORE_WIDTHS = (256, 128, 128, 128, 128, 128, 128)
 SCALAR_BANKS = (0, 3, 5)
-STORES = ((0, 1), (1, 2), (2, 4))
+STORES = ((0, 1), (1, 3), (3, 4))
 EARLY_UNITS = 2
 CASTS_BEFORE_FACTORS = 5
-POOL_WORDS = (64, 32)
+POOL_WORDS = (64, 64)
 
 
 def tile_attend_mqa_ownlists_kernel(tc, query, keys_words, keys_scales, fac, vals, offs, out):
@@ -236,13 +236,14 @@ def tile_attend_mqa_ownlists_kernel(tc, query, keys_words, keys_scales, fac, val
             nc.vector.quantize_mx(out=codes_g[:].bitcast(FP8X4), scales=scales_g[:], in_=w_bf[:])
             w_codes.append(codes_g)
             w_scales.append(scales_g)
-        quantize_units(3, UNITS - 2, "w_pairs00")
-        quantize_units(UNITS - 2, UNITS - 1, "w_bf0")
-        quantize_units(UNITS - 1, UNITS, "w_bf1")
+        quantize_units(4, UNITS - 1, "w_pairs00")
+        quantize_units(UNITS - 1, UNITS, "w_bf0")
+        quantize_units(3, 4, "w_bf1")
 
         acc = [ps.tile([P, UNIT], F32, name="acc%d" % n, tag="bank%d" % (4 + n)) for n in range(UNITS_PER_PASS)]
-        for g in range(PASSES):
-            for n in range(UNITS_PER_PASS):
+        last = UNITS_PER_PASS - 1
+        for banks in (range(last), range(last, last + 1)):
+            for g, n in [(g, n) for g in range(PASSES) for n in banks]:
                 i = g * UNITS_PER_PASS + n
                 nc.tensor.matmul_mx(
                     out=acc[n][:],
@@ -255,7 +256,7 @@ def tile_attend_mqa_ownlists_kernel(tc, query, keys_words, keys_scales, fac, val
                 )
         for first, stop in STORES:
             result = sb.tile([P, (stop - first) * UNIT], F32, name="result%d" % first)
-            copy = nc.scalar.copy if first < UNITS_PER_PASS // 2 else nc.vector.tensor_copy
+            copy = nc.vector.tensor_copy if stop - first > 1 else nc.scalar.copy
             for n in range(first, stop):
                 copy(out=result[:, (n - first) * UNIT : (n - first + 1) * UNIT], in_=acc[n][:])
             nc.sync.dma_start(out=out[:, first * UNIT : stop * UNIT], in_=result[:])

@@ -28,7 +28,7 @@ UNITS_PER_PASS = E // UNIT
 UNITS = PASSES * UNITS_PER_PASS
 HEAD_SLOTS = 160
 HEADROOM = 32.0
-Q_VECTOR = 88
+Q_VECTOR = 64
 FIRST_KEYS = 384
 SCORE_WIDTHS = (256, 128, 128, 128, 128, 128, 128)
 SCALAR_BANKS = (0, 3, 5)
@@ -52,7 +52,6 @@ def tile_attend_mqa_ownlists_kernel(tc, query, keys_words, keys_scales, fac, val
         fac_cols = sb.tile([P, PASSES, PACK], F32, name="fac_cols")
         v_raw = [sb.tile([P, PACK, 2 * UNIT], F32, name="v_raw%d" % n) for n in range(UNITS // 2)]
         ident = sb.tile([P, P], F32, name="ident")
-        placed = sb.tile([P, T], F32, name="placed")
 
         def load_values(n):
             g, h = divmod(n, 2)
@@ -76,11 +75,10 @@ def tile_attend_mqa_ownlists_kernel(tc, query, keys_words, keys_scales, fac, val
         nc.sync.dma_start(out=fac_cols[:], in_=fac[0].rearrange("(g p j) -> p g j", g=PASSES, j=PACK))
         load_values(2)
         load_values(3)
-        nc.vector.memset(placed[:], 0.0)
         nc.vector.memset(ident[:], 0.0)
         make_identity(nc, ident[:], nomemset=True)
 
-        q_bf = sb.tile([P, Q, PACK], BF16, name="q_bf", align_bytes=64)
+        q_bf = sb.tile([P, Q, PACK], BF16, name="q_bf", tag="q_bf", align_bytes=64)
         q_codes = sb.tile([P, Q], U32, name="q_codes", align_bytes=64)
         q_scales = sb.tile([P, Q], U8, name="q_scales", align_bytes=64)
         nc.vector.tensor_copy(
@@ -94,6 +92,9 @@ def tile_attend_mqa_ownlists_kernel(tc, query, keys_words, keys_scales, fac, val
         nc.vector.quantize_mx(
             out=q_codes[:].bitcast(FP8X4), scales=q_scales[:], in_=q_bf[:].rearrange("p q j -> p (q j)")
         )
+
+        placed = sb.tile([P, T], F32, name="placed", tag="q_bf", align_bytes=64)
+        nc.vector.memset(placed[:], 0.0)
 
         scores = sb.tile([P, T], F32, name="scores", tag="scores", align_bytes=64)
         start = 0
@@ -113,22 +114,18 @@ def tile_attend_mqa_ownlists_kernel(tc, query, keys_words, keys_scales, fac, val
                 stop=True,
             )
             if n in SCALAR_BANKS:
-                nc.scalar.copy(out=scores[:, cols], in_=bank[:])
+                nc.scalar.mul(out=scores[:, cols], in_=bank[:], mul=-1.0)
             else:
-                nc.vector.tensor_copy(out=scores[:, cols], in_=bank[:])
+                nc.vector.tensor_scalar_mul(scores[:, cols], bank[:], -1.0)
             start = start + width
 
         head_offsets = offsets[:, : HEAD_SLOTS // LIST_ROWS]
         rest_offsets = offsets[:, HEAD_SLOTS // LIST_ROWS :]
         negated = sb.tile([P, SLOTS], F32, name="negated", tag="negated", align_bytes=64)
         for first in (0, SLOTS // 2):
-            nc.vector.tensor_scalar(
-                out=negated[:, first : first + SLOTS // 2],
-                in0=scores[:].indirect(offsets[:, first // LIST_ROWS : (first + SLOTS // 2) // LIST_ROWS]),
-                scalar1=-1.0,
-                scalar2=0.0,
-                op0=ALU.mult,
-                op1=ALU.add,
+            nc.vector.tensor_copy(
+                negated[:, first : first + SLOTS // 2],
+                scores[:].indirect(offsets[:, first // LIST_ROWS : (first + SLOTS // 2) // LIST_ROWS]),
             )
         head_shift = sb.tile([P, 1], F32, name="head_shift", tag="head_shift", align_bytes=64)
         nc.vector.tensor_reduce(out=head_shift[:], in_=negated[:, :HEAD_SLOTS], axis=AXIS_X, op=ALU.min)

@@ -26,16 +26,16 @@ QUARTER = T // 4
 UNIT = 128
 UNITS_PER_PASS = E // UNIT
 UNITS = PASSES * UNITS_PER_PASS
-HEAD_SLOTS = 160
+HALF = SLOTS // 2
+LEAD_SLOTS = 160
 HEADROOM = 32.0
 Q_VECTOR = 64
 FIRST_KEYS = 384
 SCORE_WIDTHS = (256, 128, 128, 128, 128, 128, 128)
-SCALAR_BANKS = (0, 3, 5)
+SCALAR_BANKS = (0, 2, 4, 6)
 STORES = ((0, 1), (1, 3), (3, 4))
-EARLY_UNITS = 2
-CASTS_BEFORE_FACTORS = 5
-POOL_WORDS = (64, 64)
+POOL_WORDS = 64
+GAP_FEATURES = 64
 
 
 def tile_attend_mqa_ownlists_kernel(tc, query, keys_words, keys_scales, fac, vals, offs, out):
@@ -81,14 +81,11 @@ def tile_attend_mqa_ownlists_kernel(tc, query, keys_words, keys_scales, fac, val
         q_bf = sb.tile([P, Q, PACK], BF16, name="q_bf", tag="q_bf", align_bytes=64)
         q_codes = sb.tile([P, Q], U32, name="q_codes", align_bytes=64)
         q_scales = sb.tile([P, Q], U8, name="q_scales", align_bytes=64)
-        nc.vector.tensor_copy(
-            out=q_bf[:, :Q_VECTOR, :].rearrange("p (c i) j -> p c j i", i=4),
-            in_=q_raw[:, :, :Q_VECTOR].rearrange("p j (c i) -> p c j i", i=4),
-        )
-        nc.scalar.copy(
-            out=q_bf[:, Q_VECTOR:, :].rearrange("p (c i) j -> p c j i", i=4),
-            in_=q_raw[:, :, Q_VECTOR:].rearrange("p j (c i) -> p c j i", i=4),
-        )
+        for copy, rows in ((nc.vector.tensor_copy, slice(0, Q_VECTOR)), (nc.scalar.copy, slice(Q_VECTOR, Q))):
+            copy(
+                out=q_bf[:, rows, :].rearrange("p (c i) j -> p c j i", i=4),
+                in_=q_raw[:, :, rows].rearrange("p j (c i) -> p c j i", i=4),
+            )
         nc.vector.quantize_mx(
             out=q_codes[:].bitcast(FP8X4), scales=q_scales[:], in_=q_bf[:].rearrange("p q j -> p (q j)")
         )
@@ -119,68 +116,72 @@ def tile_attend_mqa_ownlists_kernel(tc, query, keys_words, keys_scales, fac, val
                 nc.vector.tensor_scalar_mul(scores[:, cols], bank[:], -1.0)
             start = start + width
 
-        head_offsets = offsets[:, : HEAD_SLOTS // LIST_ROWS]
-        rest_offsets = offsets[:, HEAD_SLOTS // LIST_ROWS :]
         negated = sb.tile([P, SLOTS], F32, name="negated", tag="negated", align_bytes=64)
-        for first in (0, SLOTS // 2):
-            nc.vector.tensor_copy(
-                negated[:, first : first + SLOTS // 2],
-                scores[:].indirect(offsets[:, first // LIST_ROWS : (first + SLOTS // 2) // LIST_ROWS]),
+        nc.vector.tensor_copy(negated[:, :HALF], scores[:].indirect(offsets[:, : HALF // LIST_ROWS]))
+        nc.scalar.activation(
+            out=negated[:, HALF:], in_=scores[:].indirect(offsets[:, HALF // LIST_ROWS :]), func=ACT.Copy
+        )
+        gap_bf = sb.tile([P, GAP_FEATURES, PACK], BF16, name="gap_bf", tag="scores", align_bytes=64)
+
+        def cast_values(rounded, raw):
+            nc.scalar.copy(
+                out=rounded.rearrange("p (c i) j -> p c j i", i=4),
+                in_=raw.rearrange("p j (c i) -> p c j i", i=4),
             )
-        head_shift = sb.tile([P, 1], F32, name="head_shift", tag="head_shift", align_bytes=64)
-        nc.vector.tensor_reduce(out=head_shift[:], in_=negated[:, :HEAD_SLOTS], axis=AXIS_X, op=ALU.min)
-        raised = sb.tile([P, SLOTS - HEAD_SLOTS], F32, name="raised")
+
+        cast_values(gap_bf[:], v_raw[0][:, :, :GAP_FEATURES])
+        lead_shift = sb.tile([P, 1], F32, name="lead_shift")
+        nc.vector.tensor_reduce(out=lead_shift[:], in_=negated[:, :LEAD_SLOTS], axis=AXIS_X, op=ALU.min)
+        raised = sb.tile([P, SLOTS - LEAD_SLOTS], F32, name="raised")
         rest_shift = sb.tile([P, 1], F32, name="rest_shift")
         nc.vector.tensor_scalar(
             out=raised[:],
-            in0=negated[:, HEAD_SLOTS:],
+            in0=negated[:, LEAD_SLOTS:],
             scalar1=HEADROOM,
-            scalar2=head_shift[:],
+            scalar2=lead_shift[:],
             op0=ALU.add,
             op1=ALU.min,
             accum_out=rest_shift[:],
         )
 
-        p_head = sb.tile([P, HEAD_SLOTS], F32, name="p_head")
+        p_lead = sb.tile([P, LEAD_SLOTS], F32, name="p_lead")
         p_all = sb.tile([P, SLOTS], F32, name="p_all")
         total = sb.tile([P, 1], F32, name="total", tag="total", align_bytes=64)
         inv_total = sb.tile([P, 1], F32, name="inv_total")
-        nc.scalar.activation(out=p_head[:], in_=negated[:, :HEAD_SLOTS], func=ACT.Exp, bias=head_shift[:], scale=-1.0)
+        nc.scalar.activation(out=p_lead[:], in_=negated[:, :LEAD_SLOTS], func=ACT.Exp, bias=lead_shift[:], scale=-1.0)
         nc.scalar.activation(
             out=p_all[:], in_=negated[:], func=ACT.Exp, bias=rest_shift[:], scale=-1.0, accum_out=total[:]
         )
-        nc.vector.tensor_copy(placed[:].indirect(head_offsets), p_head[:])
+        nc.vector.tensor_copy(placed[:].indirect(offsets[:, : LEAD_SLOTS // LIST_ROWS]), p_lead[:])
         nc.vector.reciprocal(out=inv_total[:], in_=total[:])
-        nc.vector.tensor_copy(placed[:].indirect(rest_offsets), p_all[:, HEAD_SLOTS:])
+        nc.vector.tensor_copy(placed[:].indirect(offsets[:, LEAD_SLOTS // LIST_ROWS :]), p_all[:, LEAD_SLOTS:])
 
-        early_bf = sb.tile([P, EARLY_UNITS, UNIT, PACK], BF16, name="early_bf", align_bytes=64)
-        late_bf = sb.tile([P, UNITS - EARLY_UNITS, UNIT, PACK], BF16, name="late_bf", tag="negated", align_bytes=64)
-        v_bf = [early_bf[:, i] if i < EARLY_UNITS else late_bf[:, i - EARLY_UNITS] for i in range(UNITS)]
+        late_bf = sb.tile([P, 2 * E, PACK], BF16, name="late_bf", tag="negated", align_bytes=64)
+        v_bf = {i: [late_bf[:, i * UNIT : (i + 1) * UNIT]] for i in range(1, UNITS)}
+        v_bf[0] = [gap_bf[:], late_bf[:, GAP_FEATURES:UNIT]]
         v_codes = sb.tile([P, UNITS * UNIT], U32, name="v_codes", align_bytes=64)
         v_scales = {}
 
-        def cast_units(first, stop):
-            for i in range(first, stop):
-                cols = slice((i % 2) * UNIT, (i % 2 + 1) * UNIT)
-                nc.scalar.copy(
-                    out=v_bf[i].rearrange("p (c i) j -> p c j i", i=4),
-                    in_=v_raw[i // 2][:, :, cols].rearrange("p j (c i) -> p c j i", i=4),
-                )
+        def cast_load(n, skip):
+            cast_values(late_bf[:, n * 2 * UNIT + skip : (n + 1) * 2 * UNIT], v_raw[n][:, :, skip:])
 
-        def quantize_units(first, stop, tag):
-            scales = sb.tile([P, (stop - first) * UNIT], U8, name="v_scales%d" % first, tag=tag, align_bytes=64)
-            for i in range(first, stop):
-                v_scales[i] = scales[:, (i - first) * UNIT : (i - first + 1) * UNIT]
-                nc.vector.quantize_mx(
-                    out=v_codes[:, i * UNIT : (i + 1) * UNIT].bitcast(FP8X4),
-                    scales=v_scales[i],
-                    in_=v_bf[i].rearrange("p e j -> p (e j)"),
-                )
+        def quantize_units(units, tag):
+            scales = sb.tile([P, len(units) * UNIT], U8, name="v_scales%d" % units[0], tag=tag, align_bytes=64)
+            for k, i in enumerate(units):
+                v_scales[i] = scales[:, k * UNIT : (k + 1) * UNIT]
+                done = 0
+                for part in v_bf[i]:
+                    width = part.shape[1]
+                    nc.vector.quantize_mx(
+                        out=v_codes[:, i * UNIT + done : i * UNIT + done + width].bitcast(FP8X4),
+                        scales=v_scales[i][:, done : done + width],
+                        in_=part.rearrange("p e j -> p (e j)"),
+                    )
+                    done = done + width
 
-        cast_units(0, CASTS_BEFORE_FACTORS)
-        quantize_units(0, 1, "scores")
-        quantize_units(1, 2, "head_shift")
-        quantize_units(2, 3, "total")
+        cast_load(0, GAP_FEATURES)
+        cast_load(1, 0)
+        quantize_units((0,), "total")
 
         fac_rows = []
         factors = []
@@ -189,11 +190,12 @@ def tile_attend_mqa_ownlists_kernel(tc, query, keys_words, keys_scales, fac, val
             for j in range(PACK):
                 nc.tensor.transpose(rows_g[:, j, :], fac_cols[:, g, j : j + 1].to_broadcast([P, P]), ident[:])
             fac_rows.append(rows_g[:].rearrange("q (u e) p -> q u p e", e=2))
-            factors.append(sb.tile([P, POOL_WORDS[g], 2], F32, name="factors%d" % g))
+            factors.append(sb.tile([P, POOL_WORDS, 2], F32, name="factors%d" % g))
             nc.scalar.activation(
-                out=factors[g][:], in_=fac_rows[g][:, 1, P - POOL_WORDS[g] :], func=ACT.Copy, scale=inv_total[:]
+                out=factors[g][:], in_=fac_rows[g][:, 1, P - POOL_WORDS :], func=ACT.Copy, scale=inv_total[:]
             )
-        cast_units(CASTS_BEFORE_FACTORS, UNITS)
+        cast_load(2, 0)
+        cast_load(3, 0)
 
         placed_v = placed[:].rearrange("q (g p u e) -> q g u p e", g=PASSES, u=2, e=2)
         turned = []
@@ -202,7 +204,7 @@ def tile_attend_mqa_ownlists_kernel(tc, query, keys_words, keys_scales, fac, val
             for u in range(2):
                 name = "w_pairs%d%d" % (g, u)
                 w_pairs = sb.tile([P, P, 2], BF16, name=name, tag=name, align_bytes=64)
-                words = P - POOL_WORDS[g] if u == 1 else P
+                words = P - POOL_WORDS if u == 1 else P
                 if u == 1:
                     nc.gpsimd.tensor_tensor(
                         out=w_pairs[:, words:], in0=placed_v[:, g, u, words:], in1=factors[g][:], op=ALU.mult
@@ -233,9 +235,9 @@ def tile_attend_mqa_ownlists_kernel(tc, query, keys_words, keys_scales, fac, val
             nc.vector.quantize_mx(out=codes_g[:].bitcast(FP8X4), scales=scales_g[:], in_=w_bf[:])
             w_codes.append(codes_g)
             w_scales.append(scales_g)
-        quantize_units(4, UNITS - 1, "w_pairs00")
-        quantize_units(UNITS - 1, UNITS, "w_bf0")
-        quantize_units(3, 4, "w_bf1")
+        quantize_units((1, 2, 4), "w_pairs00")
+        quantize_units((5, 6), "w_bf0")
+        quantize_units((3, 7), "w_bf1")
 
         acc = [ps.tile([P, UNIT], F32, name="acc%d" % n, tag="bank%d" % (4 + n)) for n in range(UNITS_PER_PASS)]
         last = UNITS_PER_PASS - 1

@@ -27,7 +27,7 @@ UNIT = 128
 UNITS_PER_PASS = E // UNIT
 UNITS = PASSES * UNITS_PER_PASS
 HALF = SLOTS // 2
-LEAD_SLOTS = 160
+LEAD_SLOTS = 128
 HEADROOM = 32.0
 Q_VECTOR = 64
 FIRST_KEYS = 384
@@ -35,7 +35,7 @@ SCORE_WIDTHS = (256, 128, 128, 128, 128, 128, 128)
 SCALAR_BANKS = (0, 2, 4, 6)
 STORES = ((0, 1), (1, 3), (3, 4))
 POOL_WORDS = 64
-GAP_FEATURES = 64
+LAST_FEATURES = 64
 
 
 def tile_attend_mqa_ownlists_kernel(tc, query, keys_words, keys_scales, fac, vals, offs, out):
@@ -117,11 +117,14 @@ def tile_attend_mqa_ownlists_kernel(tc, query, keys_words, keys_scales, fac, val
             start = start + width
 
         negated = sb.tile([P, SLOTS], F32, name="negated", tag="negated", align_bytes=64)
-        nc.vector.tensor_copy(negated[:, :HALF], scores[:].indirect(offsets[:, : HALF // LIST_ROWS]))
+        for first, stop in ((0, LEAD_SLOTS), (LEAD_SLOTS, HALF)):
+            nc.vector.tensor_copy(
+                negated[:, first:stop].bitcast(U32),
+                scores[:].bitcast(U32).indirect(offsets[:, first // LIST_ROWS : stop // LIST_ROWS]),
+            )
         nc.scalar.activation(
             out=negated[:, HALF:], in_=scores[:].indirect(offsets[:, HALF // LIST_ROWS :]), func=ACT.Copy
         )
-        gap_bf = sb.tile([P, GAP_FEATURES, PACK], BF16, name="gap_bf", tag="scores", align_bytes=64)
 
         def cast_values(rounded, raw):
             nc.scalar.copy(
@@ -129,7 +132,6 @@ def tile_attend_mqa_ownlists_kernel(tc, query, keys_words, keys_scales, fac, val
                 in_=raw.rearrange("p j (c i) -> p c j i", i=4),
             )
 
-        cast_values(gap_bf[:], v_raw[0][:, :, :GAP_FEATURES])
         lead_shift = sb.tile([P, 1], F32, name="lead_shift")
         nc.vector.tensor_reduce(out=lead_shift[:], in_=negated[:, :LEAD_SLOTS], axis=AXIS_X, op=ALU.min)
         raised = sb.tile([P, SLOTS - LEAD_SLOTS], F32, name="raised")
@@ -157,13 +159,13 @@ def tile_attend_mqa_ownlists_kernel(tc, query, keys_words, keys_scales, fac, val
         nc.vector.tensor_copy(placed[:].indirect(offsets[:, LEAD_SLOTS // LIST_ROWS :]), p_all[:, LEAD_SLOTS:])
 
         late_bf = sb.tile([P, 2 * E, PACK], BF16, name="late_bf", tag="negated", align_bytes=64)
-        v_bf = {i: [late_bf[:, i * UNIT : (i + 1) * UNIT]] for i in range(1, UNITS)}
-        v_bf[0] = [gap_bf[:], late_bf[:, GAP_FEATURES:UNIT]]
+        v_bf = {i: [late_bf[:, i * UNIT : (i + 1) * UNIT]] for i in range(UNITS)}
+        v_bf[UNITS - 1] = [late_bf[:, 2 * E - UNIT : 2 * E - LAST_FEATURES]]
         v_codes = sb.tile([P, UNITS * UNIT], U32, name="v_codes", align_bytes=64)
         v_scales = {}
 
-        def cast_load(n, skip):
-            cast_values(late_bf[:, n * 2 * UNIT + skip : (n + 1) * 2 * UNIT], v_raw[n][:, :, skip:])
+        def cast_load(n, first, stop):
+            cast_values(late_bf[:, n * 2 * UNIT + first : n * 2 * UNIT + stop], v_raw[n][:, :, first:stop])
 
         def quantize_units(units, tag):
             scales = sb.tile([P, len(units) * UNIT], U8, name="v_scales%d" % units[0], tag=tag, align_bytes=64)
@@ -179,8 +181,8 @@ def tile_attend_mqa_ownlists_kernel(tc, query, keys_words, keys_scales, fac, val
                     )
                     done = done + width
 
-        cast_load(0, GAP_FEATURES)
-        cast_load(1, 0)
+        cast_load(0, 0, 2 * UNIT)
+        cast_load(1, 0, 2 * UNIT)
         quantize_units((0,), "total")
 
         fac_rows = []
@@ -194,8 +196,8 @@ def tile_attend_mqa_ownlists_kernel(tc, query, keys_words, keys_scales, fac, val
             nc.scalar.activation(
                 out=factors[g][:], in_=fac_rows[g][:, 1, P - POOL_WORDS :], func=ACT.Copy, scale=inv_total[:]
             )
-        cast_load(2, 0)
-        cast_load(3, 0)
+        cast_load(2, 0, 2 * UNIT)
+        cast_load(3, 0, 2 * UNIT - LAST_FEATURES)
 
         placed_v = placed[:].rearrange("q (g p u e) -> q g u p e", g=PASSES, u=2, e=2)
         turned = []
@@ -235,6 +237,9 @@ def tile_attend_mqa_ownlists_kernel(tc, query, keys_words, keys_scales, fac, val
             nc.vector.quantize_mx(out=codes_g[:].bitcast(FP8X4), scales=scales_g[:], in_=w_bf[:])
             w_codes.append(codes_g)
             w_scales.append(scales_g)
+        last_bf = sb.tile([P, LAST_FEATURES, PACK], BF16, name="last_bf", tag="w_pairs11", align_bytes=64)
+        cast_values(last_bf[:], v_raw[3][:, :, 2 * UNIT - LAST_FEATURES :])
+        v_bf[UNITS - 1].append(last_bf[:])
         quantize_units((1, 2, 4), "w_pairs00")
         quantize_units((5, 6), "w_bf0")
         quantize_units((3, 7), "w_bf1")

@@ -47,7 +47,7 @@ def tile_attend_mqa_ownlists_kernel(tc, query, keys_words, keys_scales, fac, val
         offsets = sb.tile([P, SLOTS // LIST_ROWS], U16, name="offsets")
         q_raw = sb.tile([P, PACK, Q], F32, name="q_raw")
         key_cuts = ((0, FIRST_KEYS), (FIRST_KEYS, T))
-        k_words = [sb.tile([P, b - a], U32, name="k_words%d" % a, align_bytes=64) for a, b in key_cuts]
+        k_words = [sb.tile([P, b - a], U32, name="k_words%d" % a, tag="k_words%d" % a, align_bytes=64) for a, b in key_cuts]
         k_scales = sb.tile([P, QUARTER], U8, name="k_scales", align_bytes=64)
         fac_cols = sb.tile([P, PASSES, PACK], F32, name="fac_cols")
         v_raw = [sb.tile([P, PACK, 2 * UNIT], F32, name="v_raw%d" % n) for n in range(UNITS // 2)]
@@ -117,6 +117,7 @@ def tile_attend_mqa_ownlists_kernel(tc, query, keys_words, keys_scales, fac, val
             start = start + width
 
         negated = sb.tile([P, SLOTS], F32, name="negated", tag="negated", align_bytes=64)
+        first_bf = sb.tile([P, UNIT, PACK], BF16, name="first_bf", tag="k_words%d" % FIRST_KEYS, align_bytes=64)
         for first, stop in ((0, LEAD_SLOTS), (LEAD_SLOTS, HALF)):
             nc.vector.tensor_copy(
                 negated[:, first:stop].bitcast(U32),
@@ -126,12 +127,13 @@ def tile_attend_mqa_ownlists_kernel(tc, query, keys_words, keys_scales, fac, val
             out=negated[:, HALF:], in_=scores[:].indirect(offsets[:, HALF // LIST_ROWS :]), func=ACT.Copy
         )
 
-        def cast_values(rounded, raw):
-            nc.scalar.copy(
+        def cast_values(rounded, raw, copy=nc.scalar.copy):
+            copy(
                 out=rounded.rearrange("p (c i) j -> p c j i", i=4),
                 in_=raw.rearrange("p j (c i) -> p c j i", i=4),
             )
 
+        cast_values(first_bf[:], v_raw[0][:, :, :UNIT], nc.vector.tensor_copy)
         lead_shift = sb.tile([P, 1], F32, name="lead_shift")
         nc.vector.tensor_reduce(out=lead_shift[:], in_=negated[:, :LEAD_SLOTS], axis=AXIS_X, op=ALU.min)
         raised = sb.tile([P, SLOTS - LEAD_SLOTS], F32, name="raised")
@@ -159,7 +161,8 @@ def tile_attend_mqa_ownlists_kernel(tc, query, keys_words, keys_scales, fac, val
         nc.vector.tensor_copy(placed[:].indirect(offsets[:, LEAD_SLOTS // LIST_ROWS :]), p_all[:, LEAD_SLOTS:])
 
         late_bf = sb.tile([P, 2 * E, PACK], BF16, name="late_bf", tag="negated", align_bytes=64)
-        v_bf = {i: [late_bf[:, i * UNIT : (i + 1) * UNIT]] for i in range(UNITS)}
+        v_bf = {i: [late_bf[:, i * UNIT : (i + 1) * UNIT]] for i in range(1, UNITS)}
+        v_bf[0] = [first_bf[:]]
         v_bf[UNITS - 1] = [late_bf[:, 2 * E - UNIT : 2 * E - LAST_FEATURES]]
         v_codes = sb.tile([P, UNITS * UNIT], U32, name="v_codes", align_bytes=64)
         v_scales = {}
@@ -181,7 +184,7 @@ def tile_attend_mqa_ownlists_kernel(tc, query, keys_words, keys_scales, fac, val
                     )
                     done = done + width
 
-        cast_load(0, 0, 2 * UNIT)
+        cast_load(0, UNIT, 2 * UNIT)
         cast_load(1, 0, 2 * UNIT)
         quantize_units((0,), "total")
 

@@ -133,7 +133,8 @@ def tile_attend_mqa_ownlists_kernel(tc, query, keys_words, keys_scales, fac, val
                 in_=raw.rearrange("p j (c i) -> p c j i", i=4),
             )
 
-        cast_values(first_bf[:], v_raw[0][:, :, :UNIT], nc.vector.tensor_copy)
+        cast_values(first_bf[:, : UNIT // 2], v_raw[0][:, :, : UNIT // 2], nc.vector.tensor_copy)
+        cast_values(first_bf[:, UNIT // 2 :], v_raw[0][:, :, UNIT // 2 : UNIT])
         lead_shift = sb.tile([P, 1], F32, name="lead_shift")
         nc.vector.tensor_reduce(out=lead_shift[:], in_=negated[:, :LEAD_SLOTS], axis=AXIS_X, op=ALU.min)
         raised = sb.tile([P, SLOTS - LEAD_SLOTS], F32, name="raised")

@@ -36,6 +36,7 @@ SCALAR_BANKS = (0, 2, 4, 6)
 STORES = ((0, 1), (1, 3), (3, 4))
 POOL_WORDS = 64
 LAST_FEATURES = 64
+VALUE_LOADS = ((0, UNIT), (UNIT, E), (E, E + 2 * UNIT), (E + 2 * UNIT, 2 * E))
 
 
 def tile_attend_mqa_ownlists_kernel(tc, query, keys_words, keys_scales, fac, vals, offs, out):
@@ -50,12 +51,13 @@ def tile_attend_mqa_ownlists_kernel(tc, query, keys_words, keys_scales, fac, val
         k_words = [sb.tile([P, b - a], U32, name="k_words%d" % a, tag="k_words%d" % a, align_bytes=64) for a, b in key_cuts]
         k_scales = sb.tile([P, QUARTER], U8, name="k_scales", align_bytes=64)
         fac_cols = sb.tile([P, PASSES, PACK], F32, name="fac_cols")
-        v_raw = [sb.tile([P, PACK, 2 * UNIT], F32, name="v_raw%d" % n) for n in range(UNITS // 2)]
+        v_raw = [sb.tile([P, PACK, b - a], F32, name="v_raw%d" % a) for a, b in VALUE_LOADS]
         ident = sb.tile([P, P], F32, name="ident")
 
         def load_values(n):
-            g, h = divmod(n, 2)
-            rows = vals[g * K_PASS : (g + 1) * K_PASS, h * 2 * UNIT : (h + 1) * 2 * UNIT]
+            a, b = VALUE_LOADS[n]
+            g = a // E
+            rows = vals[g * K_PASS : (g + 1) * K_PASS, a - g * E : b - g * E]
             nc.sync.dma_start(out=v_raw[n][:], in_=rows.rearrange("(p j) e -> p j e", j=PACK))
 
         nc.vector.memset(k_scales[:].bitcast(I32), 0)
@@ -168,8 +170,10 @@ def tile_attend_mqa_ownlists_kernel(tc, query, keys_words, keys_scales, fac, val
         v_codes = sb.tile([P, UNITS * UNIT], U32, name="v_codes", align_bytes=64)
         v_scales = {}
 
-        def cast_load(n, first, stop):
-            cast_values(late_bf[:, n * 2 * UNIT + first : n * 2 * UNIT + stop], v_raw[n][:, :, first:stop])
+
+        def cast_load(n, kept_back):
+            a, b = VALUE_LOADS[n]
+            cast_values(late_bf[:, a : b - kept_back], v_raw[n][:, :, : b - a - kept_back])
 
         def quantize_units(units, tag):
             scales = sb.tile([P, len(units) * UNIT], U8, name="v_scales%d" % units[0], tag=tag, align_bytes=64)
@@ -185,8 +189,7 @@ def tile_attend_mqa_ownlists_kernel(tc, query, keys_words, keys_scales, fac, val
                     )
                     done = done + width
 
-        cast_load(0, UNIT, 2 * UNIT)
-        cast_load(1, 0, 2 * UNIT)
+        cast_load(1, 0)
         quantize_units((0,), "total")
 
         fac_rows = []
@@ -200,8 +203,8 @@ def tile_attend_mqa_ownlists_kernel(tc, query, keys_words, keys_scales, fac, val
             nc.scalar.activation(
                 out=factors[g][:], in_=fac_rows[g][:, 1, P - POOL_WORDS :], func=ACT.Copy, scale=inv_total[:]
             )
-        cast_load(2, 0, 2 * UNIT)
-        cast_load(3, 0, 2 * UNIT - LAST_FEATURES)
+        cast_load(2, 0)
+        cast_load(3, LAST_FEATURES)
 
         placed_v = placed[:].rearrange("q (g p u e) -> q g u p e", g=PASSES, u=2, e=2)
         turned = []

@@ -29,14 +29,14 @@ UNITS = PASSES * UNITS_PER_PASS
 HALF = SLOTS // 2
 LEAD_SLOTS = 128
 HEADROOM = 32.0
-Q_VECTOR = 64
-FIRST_KEYS = 384
+Q_VECTOR = 80
+KEY_CUTS = ((0, 256), (256, 640), (640, T))
 SCORE_WIDTHS = (256, 128, 128, 128, 128, 128, 128)
 SCALAR_BANKS = (0, 2, 4, 6)
 STORES = ((0, 1), (1, 3), (3, 4))
 POOL_WORDS = 64
 LAST_FEATURES = 64
-VALUE_LOADS = ((0, UNIT), (UNIT, E), (E, E + 2 * UNIT), (E + 2 * UNIT, 2 * E))
+VALUE_LOADS = ((0, UNIT), (UNIT, E), (E, 2 * E))
 
 
 def tile_attend_mqa_ownlists_kernel(tc, query, keys_words, keys_scales, fac, vals, offs, out):
@@ -47,8 +47,7 @@ def tile_attend_mqa_ownlists_kernel(tc, query, keys_words, keys_scales, fac, val
 
         offsets = sb.tile([P, SLOTS // LIST_ROWS], U16, name="offsets")
         q_raw = sb.tile([P, PACK, Q], F32, name="q_raw")
-        key_cuts = ((0, FIRST_KEYS), (FIRST_KEYS, T))
-        k_words = [sb.tile([P, b - a], U32, name="k_words%d" % a, tag="k_words%d" % a, align_bytes=64) for a, b in key_cuts]
+        k_words = [sb.tile([P, b - a], U32, name="k_words%d" % a, tag="k_words%d" % a, align_bytes=64) for a, b in KEY_CUTS]
         k_scales = sb.tile([P, QUARTER], U8, name="k_scales", align_bytes=64)
         fac_cols = sb.tile([P, PASSES, PACK], F32, name="fac_cols")
         v_raw = [sb.tile([P, PACK, b - a], F32, name="v_raw%d" % a) for a, b in VALUE_LOADS]
@@ -63,34 +62,37 @@ def tile_attend_mqa_ownlists_kernel(tc, query, keys_words, keys_scales, fac, val
         nc.vector.memset(k_scales[:].bitcast(I32), 0)
         nc.sync.dma_start(out=q_raw[:], in_=query.rearrange("(p j) q -> p j q", j=PACK))
         key_ints = keys_words[0].rearrange("p n t -> p (n t)").bitcast(I32)
-        nc.sync.dma_start(out=k_words[0][:].bitcast(I32), in_=key_ints[:, :FIRST_KEYS])
+        nc.sync.dma_start(out=k_words[0][:].bitcast(I32), in_=key_ints[:, : KEY_CUTS[0][1]])
         scale_words = keys_scales[0].bitcast(I32)
         for quad in range(4):
             nc.sync.dma_start(
                 out=k_scales[32 * quad : 32 * quad + 16, :].bitcast(I32),
                 in_=scale_words[4 * quad : 4 * quad + 4, :].rearrange("r (h c) -> h r c", h=4),
             )
-        nc.sync.dma_start(out=k_words[1][:].bitcast(I32), in_=key_ints[:, FIRST_KEYS:])
+        for piece in (1, 2):
+            nc.sync.dma_start(out=k_words[piece][:].bitcast(I32), in_=key_ints[:, slice(*KEY_CUTS[piece])])
         load_values(0)
         nc.sync.dma_start(offsets[:], offs)
         load_values(1)
         nc.sync.dma_start(out=fac_cols[:], in_=fac[0].rearrange("(g p j) -> p g j", g=PASSES, j=PACK))
         load_values(2)
-        load_values(3)
         nc.vector.memset(ident[:], 0.0)
         make_identity(nc, ident[:], nomemset=True)
 
         q_bf = sb.tile([P, Q, PACK], BF16, name="q_bf", tag="q_bf", align_bytes=64)
         q_codes = sb.tile([P, Q], U32, name="q_codes", align_bytes=64)
         q_scales = sb.tile([P, Q], U8, name="q_scales", align_bytes=64)
-        for copy, rows in ((nc.vector.tensor_copy, slice(0, Q_VECTOR)), (nc.scalar.copy, slice(Q_VECTOR, Q))):
+        for copy, rows in ((nc.vector.tensor_copy, slice(0, 64)), (nc.vector.tensor_copy, slice(64, Q_VECTOR)), (nc.scalar.copy, slice(Q_VECTOR, Q))):
             copy(
                 out=q_bf[:, rows, :].rearrange("p (c i) j -> p c j i", i=4),
                 in_=q_raw[:, :, rows].rearrange("p j (c i) -> p c j i", i=4),
             )
-        nc.vector.quantize_mx(
-            out=q_codes[:].bitcast(FP8X4), scales=q_scales[:], in_=q_bf[:].rearrange("p q j -> p (q j)")
-        )
+        for rows in (slice(0, 64), slice(64, Q)):
+            nc.vector.quantize_mx(
+                out=q_codes[:, rows].bitcast(FP8X4),
+                scales=q_scales[:, rows],
+                in_=q_bf[:, rows, :].rearrange("p q j -> p (q j)"),
+            )
 
         placed = sb.tile([P, T], F32, name="placed", tag="q_bf", align_bytes=64)
         nc.vector.memset(placed[:], 0.0)
@@ -100,8 +102,8 @@ def tile_attend_mqa_ownlists_kernel(tc, query, keys_words, keys_scales, fac, val
         for n, width in enumerate(SCORE_WIDTHS):
             cols = slice(start, start + width)
             quarter, in_quarter = divmod(start, QUARTER)
-            piece = 0 if start < FIRST_KEYS else 1
-            in_piece = start - key_cuts[piece][0]
+            piece = [start < stop for first, stop in KEY_CUTS].index(True)
+            in_piece = start - KEY_CUTS[piece][0]
             bank = ps.tile([P, width], F32, name="score_bank%d" % n, tag="bank%d" % n)
             nc.tensor.matmul_mx(
                 out=bank[:],
@@ -119,7 +121,7 @@ def tile_attend_mqa_ownlists_kernel(tc, query, keys_words, keys_scales, fac, val
             start = start + width
 
         negated = sb.tile([P, SLOTS], F32, name="negated", tag="negated", align_bytes=64)
-        first_bf = sb.tile([P, UNIT, PACK], BF16, name="first_bf", tag="k_words%d" % FIRST_KEYS, align_bytes=64)
+        first_bf = sb.tile([P, UNIT, PACK], BF16, name="first_bf", tag="k_words%d" % KEY_CUTS[2][0], align_bytes=64)
         for first, stop in ((0, LEAD_SLOTS), (LEAD_SLOTS, HALF)):
             nc.vector.tensor_copy(
                 negated[:, first:stop].bitcast(U32),
@@ -203,8 +205,8 @@ def tile_attend_mqa_ownlists_kernel(tc, query, keys_words, keys_scales, fac, val
             nc.scalar.activation(
                 out=factors[g][:], in_=fac_rows[g][:, 1, P - POOL_WORDS :], func=ACT.Copy, scale=inv_total[:]
             )
-        cast_load(2, 0)
-        cast_load(3, LAST_FEATURES)
+        cast_values(late_bf[:, E : E + 2 * UNIT], v_raw[2][:, :, : 2 * UNIT])
+        cast_values(late_bf[:, E + 2 * UNIT : 2 * E - LAST_FEATURES], v_raw[2][:, :, 2 * UNIT : E - LAST_FEATURES])
 
         placed_v = placed[:].rearrange("q (g p u e) -> q g u p e", g=PASSES, u=2, e=2)
         turned = []
@@ -245,7 +247,7 @@ def tile_attend_mqa_ownlists_kernel(tc, query, keys_words, keys_scales, fac, val
             w_codes.append(codes_g)
             w_scales.append(scales_g)
         last_bf = sb.tile([P, LAST_FEATURES, PACK], BF16, name="last_bf", tag="w_pairs11", align_bytes=64)
-        cast_values(last_bf[:], v_raw[3][:, :, 2 * UNIT - LAST_FEATURES :])
+        cast_values(last_bf[:], v_raw[2][:, :, E - LAST_FEATURES :])
         v_bf[UNITS - 1].append(last_bf[:])
         quantize_units((1, 2, 4), "w_pairs00")
         quantize_units((5, 6), "w_bf0")

@@ -30,9 +30,9 @@ HALF = SLOTS // 2
 LEAD_SLOTS = 128
 HEADROOM = 32.0
 Q_VECTOR = 80
-KEY_CUTS = ((0, 256), (256, 640), (640, T))
-SCORE_WIDTHS = (256, 128, 128, 128, 128, 128, 128)
-SCALAR_BANKS = (0, 2, 4, 6)
+KEY_CUTS = ((0, 256), (256, 768), (768, T))
+SCORE_WIDTHS = (256, 256, 256, 128, 128)
+SCALAR_BANKS = (1, 3, 4)
 STORES = ((0, 1), (1, 3), (3, 4))
 POOL_WORDS = 64
 LAST_FEATURES = 64

@@ -139,7 +139,7 @@ def tile_attend_mqa_ownlists_kernel(tc, query, keys_words, keys_scales, fac, val
 
         cast_values(first_bf[:, : UNIT // 2], v_raw[0][:, :, : UNIT // 2], nc.vector.tensor_copy)
         cast_values(first_bf[:, UNIT // 2 :], v_raw[0][:, :, UNIT // 2 : UNIT])
-        lead_shift = sb.tile([P, 1], F32, name="lead_shift")
+        lead_shift = sb.tile([P, 1], F32, name="lead_shift", tag="lead_shift", align_bytes=64)
         nc.vector.tensor_reduce(out=lead_shift[:], in_=negated[:, :LEAD_SLOTS], axis=AXIS_X, op=ALU.min)
         raised = sb.tile([P, SLOTS - LEAD_SLOTS], F32, name="raised")
         rest_shift = sb.tile([P, 1], F32, name="rest_shift")
@@ -173,10 +173,6 @@ def tile_attend_mqa_ownlists_kernel(tc, query, keys_words, keys_scales, fac, val
         v_scales = {}
 
 
-        def cast_load(n, kept_back):
-            a, b = VALUE_LOADS[n]
-            cast_values(late_bf[:, a : b - kept_back], v_raw[n][:, :, : b - a - kept_back])
-
         def quantize_units(units, tag):
             scales = sb.tile([P, len(units) * UNIT], U8, name="v_scales%d" % units[0], tag=tag, align_bytes=64)
             for k, i in enumerate(units):
@@ -191,8 +187,10 @@ def tile_attend_mqa_ownlists_kernel(tc, query, keys_words, keys_scales, fac, val
                     )
                     done = done + width
 
-        cast_load(1, 0)
-        quantize_units((0,), "total")
+        cast_values(late_bf[:, UNIT : 2 * UNIT], v_raw[1][:, :, :UNIT])
+        cast_values(late_bf[:, 2 * UNIT : E], v_raw[1][:, :, UNIT:])
+        quantize_units((0,), "lead_shift")
+        quantize_units((1,), "total")
 
         fac_rows = []
         factors = []
@@ -249,8 +247,7 @@ def tile_attend_mqa_ownlists_kernel(tc, query, keys_words, keys_scales, fac, val
         last_bf = sb.tile([P, LAST_FEATURES, PACK], BF16, name="last_bf", tag="w_pairs11", align_bytes=64)
         cast_values(last_bf[:], v_raw[2][:, :, E - LAST_FEATURES :])
         v_bf[UNITS - 1].append(last_bf[:])
-        quantize_units((1, 2, 4), "w_pairs00")
-        quantize_units((5, 6), "w_bf0")
+        quantize_units((2, 4, 5, 6), "w_pairs00")
         quantize_units((3, 7), "w_bf1")
 
         acc = [ps.tile([P, UNIT], F32, name="acc%d" % n, tag="bank%d" % (4 + n)) for n in range(UNITS_PER_PASS)]

from contextlib import ExitStack

import concourse.mybir as mybir
from concourse.masks import make_identity

D, T, Q, SLOTS, E = 512, 1024, 128, 512, 512
FLOPS = 2 * Q * D * T + 2 * Q * T * E

F32 = mybir.dt.float32
BF16 = mybir.dt.bfloat16
I32 = mybir.dt.int32
U32 = mybir.dt.uint32
U16 = mybir.dt.uint16
U8 = mybir.dt.uint8
FP8X4 = mybir.dt.float8_e4m3fn_x4
ALU = mybir.AluOpType
ACT = mybir.ActivationFunctionType
AXIS_X = mybir.AxisListType.X

P = 128
PACK = 4
K_PASS = P * PACK
PASSES = T // K_PASS
LIST_ROWS = 16
QUARTER = T // 4
UNIT = 128
UNITS_PER_PASS = E // UNIT
UNITS = PASSES * UNITS_PER_PASS
HALF = SLOTS // 2
LEAD_SLOTS = 128
HEADROOM = 32.0
Q_VECTOR = 80
KEY_CUTS = ((0, 256), (256, 768), (768, T))
SCORE_WIDTHS = (256, 256, 256, 128, 128)
SCALAR_BANKS = (1, 3, 4)
STORES = ((0, 1), (1, 3), (3, 4))
POOL_WORDS = 64
LAST_FEATURES = 64
VALUE_LOADS = ((0, UNIT), (UNIT, E), (E, 2 * E))


def tile_attend_mqa_ownlists_kernel(tc, query, keys_words, keys_scales, fac, vals, offs, out):
    nc = tc.nc
    with ExitStack() as ctx:
        sb = ctx.enter_context(tc.tile_pool(name="sb", bufs=1))
        ps = ctx.enter_context(tc.psum_pool(name="ps", bufs=1))

        offsets = sb.tile([P, SLOTS // LIST_ROWS], U16, name="offsets")
        q_raw = sb.tile([P, PACK, Q], F32, name="q_raw")
        k_words = [sb.tile([P, b - a], U32, name="k_words%d" % a, tag="k_words%d" % a, align_bytes=64) for a, b in KEY_CUTS]
        k_scales = sb.tile([P, QUARTER], U8, name="k_scales", align_bytes=64)
        fac_cols = sb.tile([P, PASSES, PACK], F32, name="fac_cols")
        v_raw = [sb.tile([P, PACK, b - a], F32, name="v_raw%d" % a) for a, b in VALUE_LOADS]
        ident = sb.tile([P, P], F32, name="ident")

        def load_values(n):
            a, b = VALUE_LOADS[n]
            g = a // E
            rows = vals[g * K_PASS : (g + 1) * K_PASS, a - g * E : b - g * E]
            nc.sync.dma_start(out=v_raw[n][:], in_=rows.rearrange("(p j) e -> p j e", j=PACK))

        nc.vector.memset(k_scales[:].bitcast(I32), 0)
        nc.sync.dma_start(out=q_raw[:], in_=query.rearrange("(p j) q -> p j q", j=PACK))
        key_ints = keys_words[0].rearrange("p n t -> p (n t)").bitcast(I32)
        nc.sync.dma_start(out=k_words[0][:].bitcast(I32), in_=key_ints[:, : KEY_CUTS[0][1]])
        scale_words = keys_scales[0].bitcast(I32)
        for quad in range(4):
            nc.sync.dma_start(
                out=k_scales[32 * quad : 32 * quad + 16, :].bitcast(I32),
                in_=scale_words[4 * quad : 4 * quad + 4, :].rearrange("r (h c) -> h r c", h=4),
            )
        for piece in (1, 2):
            nc.sync.dma_start(out=k_words[piece][:].bitcast(I32), in_=key_ints[:, slice(*KEY_CUTS[piece])])
        load_values(0)
        nc.sync.dma_start(offsets[:], offs)
        load_values(1)
        nc.sync.dma_start(out=fac_cols[:], in_=fac[0].rearrange("(g p j) -> p g j", g=PASSES, j=PACK))
        load_values(2)
        nc.vector.memset(ident[:], 0.0)
        make_identity(nc, ident[:], nomemset=True)

        q_bf = sb.tile([P, Q, PACK], BF16, name="q_bf", tag="q_bf", align_bytes=64)
        q_codes = sb.tile([P, Q], U32, name="q_codes", align_bytes=64)
        q_scales = sb.tile([P, Q], U8, name="q_scales", align_bytes=64)
        for copy, rows in ((nc.vector.tensor_copy, slice(0, 64)), (nc.vector.tensor_copy, slice(64, Q_VECTOR)), (nc.scalar.copy, slice(Q_VECTOR, Q))):
            copy(
                out=q_bf[:, rows, :].rearrange("p (c i) j -> p c j i", i=4),
                in_=q_raw[:, :, rows].rearrange("p j (c i) -> p c j i", i=4),
            )
        for rows in (slice(0, 64), slice(64, Q)):
            nc.vector.quantize_mx(
                out=q_codes[:, rows].bitcast(FP8X4),
                scales=q_scales[:, rows],
                in_=q_bf[:, rows, :].rearrange("p q j -> p (q j)"),
            )

        placed = sb.tile([P, T], F32, name="placed", tag="q_bf", align_bytes=64)
        nc.vector.memset(placed[:], 0.0)

        scores = sb.tile([P, T], F32, name="scores", tag="scores", align_bytes=64)
        start = 0
        for n, width in enumerate(SCORE_WIDTHS):
            cols = slice(start, start + width)
            quarter, in_quarter = divmod(start, QUARTER)
            piece = [start < stop for first, stop in KEY_CUTS].index(True)
            in_piece = start - KEY_CUTS[piece][0]
            bank = ps.tile([P, width], F32, name="score_bank%d" % n, tag="bank%d" % n)
            nc.tensor.matmul_mx(
                out=bank[:],
                lhsT=q_codes[:].bitcast(FP8X4),
                lhsT_scale=q_scales[:],
                rhs=k_words[piece][:, in_piece : in_piece + width].bitcast(FP8X4),
                rhs_scale=k_scales[4 * quarter : P, in_quarter : in_quarter + width],
                start=True,
                stop=True,
            )
            if n in SCALAR_BANKS:
                nc.scalar.mul(out=scores[:, cols], in_=bank[:], mul=-1.0)
            else:
                nc.vector.tensor_scalar_mul(scores[:, cols], bank[:], -1.0)
            start = start + width

        negated = sb.tile([P, SLOTS], F32, name="negated", tag="negated", align_bytes=64)
        first_bf = sb.tile([P, UNIT, PACK], BF16, name="first_bf", tag="k_words%d" % KEY_CUTS[2][0], align_bytes=64)
        for first, stop in ((0, LEAD_SLOTS), (LEAD_SLOTS, HALF)):
            nc.vector.tensor_copy(
                negated[:, first:stop].bitcast(U32),
                scores[:].bitcast(U32).indirect(offsets[:, first // LIST_ROWS : stop // LIST_ROWS]),
            )
        nc.scalar.activation(
            out=negated[:, HALF:], in_=scores[:].indirect(offsets[:, HALF // LIST_ROWS :]), func=ACT.Copy
        )

        def cast_values(rounded, raw, copy=nc.scalar.copy):
            copy(
                out=rounded.rearrange("p (c i) j -> p c j i", i=4),
                in_=raw.rearrange("p j (c i) -> p c j i", i=4),
            )

        cast_values(first_bf[:, : UNIT // 2], v_raw[0][:, :, : UNIT // 2], nc.vector.tensor_copy)
        cast_values(first_bf[:, UNIT // 2 :], v_raw[0][:, :, UNIT // 2 : UNIT])
        lead_shift = sb.tile([P, 1], F32, name="lead_shift", tag="lead_shift", align_bytes=64)
        nc.vector.tensor_reduce(out=lead_shift[:], in_=negated[:, :LEAD_SLOTS], axis=AXIS_X, op=ALU.min)
        raised = sb.tile([P, SLOTS - LEAD_SLOTS], F32, name="raised")
        rest_shift = sb.tile([P, 1], F32, name="rest_shift")
        nc.vector.tensor_scalar(
            out=raised[:],
            in0=negated[:, LEAD_SLOTS:],
            scalar1=HEADROOM,
            scalar2=lead_shift[:],
            op0=ALU.add,
            op1=ALU.min,
            accum_out=rest_shift[:],
        )

        p_lead = sb.tile([P, LEAD_SLOTS], F32, name="p_lead")
        p_all = sb.tile([P, SLOTS], F32, name="p_all")
        total = sb.tile([P, 1], F32, name="total", tag="total", align_bytes=64)
        inv_total = sb.tile([P, 1], F32, name="inv_total")
        nc.scalar.activation(out=p_lead[:], in_=negated[:, :LEAD_SLOTS], func=ACT.Exp, bias=lead_shift[:], scale=-1.0)
        nc.scalar.activation(
            out=p_all[:], in_=negated[:], func=ACT.Exp, bias=rest_shift[:], scale=-1.0, accum_out=total[:]
        )
        nc.vector.tensor_copy(placed[:].indirect(offsets[:, : LEAD_SLOTS // LIST_ROWS]), p_lead[:])
        nc.vector.reciprocal(out=inv_total[:], in_=total[:])
        nc.vector.tensor_copy(placed[:].indirect(offsets[:, LEAD_SLOTS // LIST_ROWS :]), p_all[:, LEAD_SLOTS:])

        late_bf = sb.tile([P, 2 * E, PACK], BF16, name="late_bf", tag="negated", align_bytes=64)
        v_bf = {i: [late_bf[:, i * UNIT : (i + 1) * UNIT]] for i in range(1, UNITS)}
        v_bf[0] = [first_bf[:]]
        v_bf[UNITS - 1] = [late_bf[:, 2 * E - UNIT : 2 * E - LAST_FEATURES]]
        v_codes = sb.tile([P, UNITS * UNIT], U32, name="v_codes", align_bytes=64)
        v_scales = {}


        def quantize_units(units, tag):
            scales = sb.tile([P, len(units) * UNIT], U8, name="v_scales%d" % units[0], tag=tag, align_bytes=64)
            for k, i in enumerate(units):
                v_scales[i] = scales[:, k * UNIT : (k + 1) * UNIT]
                done = 0
                for part in v_bf[i]:
                    width = part.shape[1]
                    nc.vector.quantize_mx(
                        out=v_codes[:, i * UNIT + done : i * UNIT + done + width].bitcast(FP8X4),
                        scales=v_scales[i][:, done : done + width],
                        in_=part.rearrange("p e j -> p (e j)"),
                    )
                    done = done + width

        cast_values(late_bf[:, UNIT : 2 * UNIT], v_raw[1][:, :, :UNIT])
        cast_values(late_bf[:, 2 * UNIT : E], v_raw[1][:, :, UNIT:])
        quantize_units((0,), "lead_shift")
        quantize_units((1,), "total")

        fac_rows = []
        factors = []
        for g in range(PASSES):
            rows_g = ps.tile([P, PACK, P], F32, name="fac_rows%d" % g, tag="bank%d" % g)
            for j in range(PACK):
                nc.tensor.transpose(rows_g[:, j, :], fac_cols[:, g, j : j + 1].to_broadcast([P, P]), ident[:])
            fac_rows.append(rows_g[:].rearrange("q (u e) p -> q u p e", e=2))
            factors.append(sb.tile([P, POOL_WORDS, 2], F32, name="factors%d" % g))
            nc.scalar.activation(
                out=factors[g][:], in_=fac_rows[g][:, 1, P - POOL_WORDS :], func=ACT.Copy, scale=inv_total[:]
            )
        cast_values(late_bf[:, E : E + 2 * UNIT], v_raw[2][:, :, : 2 * UNIT])
        cast_values(late_bf[:, E + 2 * UNIT : 2 * E - LAST_FEATURES], v_raw[2][:, :, 2 * UNIT : E - LAST_FEATURES])

        placed_v = placed[:].rearrange("q (g p u e) -> q g u p e", g=PASSES, u=2, e=2)
        turned = []
        for g in range(PASSES):
            turned_g = ps.tile([P, 2, Q], F32, name="turned%d" % g, tag="bank%d" % (2 + g))
            for u in range(2):
                name = "w_pairs%d%d" % (g, u)
                w_pairs = sb.tile([P, P, 2], BF16, name=name, tag=name, align_bytes=64)
                words = P - POOL_WORDS if u == 1 else P
                if u == 1:
                    nc.gpsimd.tensor_tensor(
                        out=w_pairs[:, words:], in0=placed_v[:, g, u, words:], in1=factors[g][:], op=ALU.mult
                    )
                nc.vector.scalar_tensor_tensor(
                    out=w_pairs[:, :words],
                    in0=placed_v[:, g, u, :words],
                    scalar=inv_total[:],
                    in1=fac_rows[g][:, u, :words],
                    op0=ALU.mult,
                    op1=ALU.mult,
                )
                nc.tensor.transpose(
                    turned_g[:, u, :], w_pairs[:].rearrange("q p e -> q (p e)").bitcast(F32), ident[:]
                )
            turned.append(turned_g)

        w_codes = []
        w_scales = []
        for g in range(PASSES):
            w_bf = sb.tile([P, Q * PACK], BF16, name="w_bf%d" % g, tag="w_bf%d" % g, align_bytes=64)
            nc.scalar.copy(
                out=w_bf[:].bitcast(F32).rearrange("p (q u) -> p q u", u=2),
                in_=turned[g][:].rearrange("p u q -> p q u"),
            )
            codes_g = sb.tile([P, Q], U32, name="w_codes%d" % g, align_bytes=64)
            scales_g = sb.tile([P, Q], U8, name="w_scales%d" % g, align_bytes=64)
            nc.vector.quantize_mx(out=codes_g[:].bitcast(FP8X4), scales=scales_g[:], in_=w_bf[:])
            w_codes.append(codes_g)
            w_scales.append(scales_g)
        last_bf = sb.tile([P, LAST_FEATURES, PACK], BF16, name="last_bf", tag="w_pairs11", align_bytes=64)
        cast_values(last_bf[:], v_raw[2][:, :, E - LAST_FEATURES :])
        v_bf[UNITS - 1].append(last_bf[:])
        quantize_units((2, 4, 5, 6), "w_pairs00")
        quantize_units((3, 7), "w_bf1")

        acc = [ps.tile([P, UNIT], F32, name="acc%d" % n, tag="bank%d" % (4 + n)) for n in range(UNITS_PER_PASS)]
        last = UNITS_PER_PASS - 1
        for banks in (range(last), range(last, last + 1)):
            for g, n in [(g, n) for g in range(PASSES) for n in banks]:
                i = g * UNITS_PER_PASS + n
                nc.tensor.matmul_mx(
                    out=acc[n][:],
                    lhsT=w_codes[g][:].bitcast(FP8X4),
                    lhsT_scale=w_scales[g][:],
                    rhs=v_codes[:, i * UNIT : (i + 1) * UNIT].bitcast(FP8X4),
                    rhs_scale=v_scales[i],
                    start=(g == 0),
                    stop=(g == PASSES - 1),
                )
        for first, stop in STORES:
            result = sb.tile([P, (stop - first) * UNIT], F32, name="result%d" % first)
            copy = nc.vector.tensor_copy if stop - first > 1 else nc.scalar.copy
            for n in range(first, stop):
                copy(out=result[:, (n - first) * UNIT : (n - first + 1) * UNIT], in_=acc[n][:])
            nc.sync.dma_start(out=out[:, first * UNIT : stop * UNIT], in_=result[:])
